import numpy as np
import ml_dtypes


def mxq(x, axis, fmt="e4m3"):
    dtype, down = {"e4m3": (ml_dtypes.float8_e4m3fn, 7), "e5m2": (ml_dtypes.float8_e5m2, 14)}[fmt]
    v = np.moveaxis(np.asarray(x, np.float32).astype(ml_dtypes.bfloat16).astype(np.float64), axis, -1)
    blocks = v.reshape(v.shape[:-1] + (-1, 32))
    amax = np.abs(blocks).max(-1, keepdims=True)
    byte = np.maximum(np.where(amax > 0, np.frexp(amax)[1] - 1 + 127, 0) - down, 1)
    scale = np.exp2(byte - 127.0)
    codes = (blocks / scale).astype(np.float32).astype(dtype).astype(np.float64)
    return np.moveaxis((codes * scale).reshape(v.shape), -1, axis)


WIDE = False


def mx_kscale(k):
    if not WIDE:
        return np.ones(k)
    levels = np.array([10, -10, 5, -5, 0])
    if k % 512:
        return np.exp2(np.random.permutation(np.resize(levels, k // 32))).repeat(32)
    a = np.empty((k // 512, 16))
    for p in range(k // 512):
        a[p, :8] = np.random.permutation(np.resize(levels, 8))
        for g in range(8):
            far = levels[np.abs(levels - a[p, g]) >= 10]
            a[p, g + 8] = far[np.random.randint(len(far))]
    return np.exp2(a.ravel()).repeat(32)


BF16 = ml_dtypes.bfloat16


def bf(x):
    return np.asarray(x, np.float32).astype(BF16)


def f64(x):
    return np.asarray(x).astype(np.float64)


E2M1 = np.array([0.0, 0.5, 1.0, 1.5, 2.0, 3.0, 4.0, 6.0, -0.0, -0.5, -1.0, -1.5, -2.0, -3.0, -4.0, -6.0])


def pack_weight(w, fmt):
    k, n = w.shape
    w = f64(bf(w)).reshape(k // 32, 32, n)
    amax = np.abs(w).max(1)
    if fmt == "e4m3":
        byte = np.frexp(amax)[1] - 1 + 127 - 7
    else:
        mant, ex = np.frexp(amax / 6.0)
        byte = np.where(mant > 0.5, ex, ex - 1) + 127
    byte = np.clip(np.where(amax > 0, byte, 1), 1, 254)
    scaled = (w * np.exp2(127.0 - byte)[:, None, :]).reshape(k, n).astype(np.float32)
    by_word = np.ascontiguousarray(scaled.reshape(k // 512, 128, 4, n).transpose(0, 1, 3, 2))
    if fmt == "e4m3":
        words = by_word.astype(ml_dtypes.float8_e4m3fn).view(np.uint8)
    else:
        c = by_word.astype(ml_dtypes.float4_e2m1fn).view(np.uint8) & 0xF
        words = c[..., 0::2] | (c[..., 1::2] << 4)
    return np.ascontiguousarray(words), np.ascontiguousarray(byte.astype(np.uint8).reshape(k // 512, 16, n))


def unpack_weight(words, scales, fmt):
    g, p, n, _ = words.shape
    if fmt == "e4m3":
        vals = np.ascontiguousarray(words).view(ml_dtypes.float8_e4m3fn).astype(np.float64)
    else:
        nib = np.empty((g, p, n, 4), np.uint8)
        nib[..., 0::2] = words & 0xF
        nib[..., 1::2] = words >> 4
        vals = E2M1[nib]
    vals = vals * np.repeat(np.exp2(scales.astype(np.float64) - 127.0), 8, axis=1)[..., None]
    return vals.transpose(0, 1, 3, 2).reshape(g * 512, n)

E4M3FN = np.array([(-1.0 if i & 128 else 1.0) * ((1.0 + (i & 7) / 8.0) * 2.0 ** (((i >> 3) & 15) - 7) if i & 120 else (i & 7) * 2.0 ** -9) for i in range(256)])


def e4m3fn_bytes(y):
    return np.clip(np.asarray(y, np.float64), -448.0, 448.0).astype(np.float32).astype(ml_dtypes.float8_e4m3fn).view(np.uint8)


def e4m3fn_values(b):
    return E4M3FN[b]


T, D, R, N = 1024, 1024, 512, 1024


def masked_coupling(m, pattern):
    return np.where(pattern < 0.25, m, np.zeros_like(m))


def draw0():
    s, r, t = mx_kscale(D), mx_kscale(R), mx_kscale(R)
    x = bf(np.random.standard_normal((T, D)) * s)
    w0_words, w0_scales = pack_weight(np.random.standard_normal((D, N)) / np.sqrt(D) / s[:, None], "e4m3")
    u_words, u_scales = pack_weight(np.random.standard_normal((D, R)) / np.sqrt(D) / s[:, None] * t, "e4m3")
    m = bf(np.random.standard_normal((R, R)) * 2.0 / np.sqrt(R) * r / t[:, None])
    pattern = bf(np.random.uniform(0.0, 1.0, (R, R)))
    vt_words, vt_scales = pack_weight(np.random.standard_normal((R, N)) / np.sqrt(R) / r[:, None], "e4m3")
    return {"x": x,
            "w0_words": w0_words, "w0_scales": w0_scales,
            "u_words": u_words, "u_scales": u_scales,
            "m": m,
            "pattern": pattern,
            "vt_words": vt_words, "vt_scales": vt_scales}


def core(x, w0_words, w0_scales, u_words, u_scales, m, pattern, vt_words, vt_scales):
    xq = mxq(f64(x), 1, "e4m3")
    ms = masked_coupling(f64(m), f64(pattern))
    n = mxq(ms, 1, "e4m3") @ unpack_weight(vt_words, vt_scales, "e4m3")
    h = xq @ unpack_weight(u_words, u_scales, "e4m3")
    d = mxq(h, 1, "e4m3") @ mxq(n, 0, "e4m3")
    b = xq @ unpack_weight(w0_words, w0_scales, "e4m3")
    y = b + d
    return y


def setup_inputs():
    drawn = draw0()
    full = np.asarray(drawn['x']).astype(np.float64)
    scale = (np.abs(full).reshape(1024, 8, 128).max(axis=(2,)) / 448.0).astype(np.float32)
    given = {}
    for key, value in drawn.items():
        if key == 'x':
            given['x_bytes'] = e4m3fn_bytes(full / np.repeat(scale.astype(np.float64), 128, axis=1))
            given['x_scale'] = scale
        else:
            given[key] = value
    return given


def reference(x_bytes, x_scale, w0_words, w0_scales, u_words, u_scales, m, pattern, vt_words, vt_scales):
    return core(e4m3fn_values(x_bytes) * np.repeat(x_scale.astype(np.float64), 128, axis=1), w0_words, w0_scales, u_words, u_scales, m, pattern, vt_words, vt_scales)

@@ -1,0 +1,348 @@
+from contextlib import ExitStack
+
+import concourse.mybir as mybir
+from concourse.masks import make_identity
+
+T, D, R, N = 1024, 1024, 512, 1024
+FLOPS = 2 * (R * R * N + T * D * R + T * R * N + T * D * N)
+
+P = 128
+F32 = mybir.dt.float32
+BF16 = mybir.dt.bfloat16
+I32 = mybir.dt.int32
+U32 = mybir.dt.uint32
+U8 = mybir.dt.uint8
+FP8 = mybir.dt.float8_e4m3fn
+X4 = mybir.dt.float8_e4m3fn_x4
+ALU = mybir.AluOpType
+ACT = mybir.ActivationFunctionType
+
+ORDER = (
+    "Wa.0.v Wb.0.s Wa.1.v Wb.1.v Ma.0.- T.0.- C.0.v Ma.1.- Mb.0.- Mb.1.- Q.0.- T.1.- Tm.0.- C.1.s Wb.2.s "
+    "Tm.1.- Cm.0.s Cm.1.s Wa.2.v Q.1.- Wb.3.v Ba.0.- T.2.- C.2.s Wa.3.v T.3.- Qm.0.- C.3.s UP.0.- Ba.1.- "
+    "N.0.- Q.2.- N.1.- N.2.- CN.0.s CN.1.v Q.3.- CN.2.s H.0.- N.3.- H.1.- D.0.s Wa.4.v Wa.5.v N.4.- "
+    "CN.3.s N.5.- QN.0.- QN.1.- I.0.- Wb.4.v D.1.s Wb.5.v Bb.0.- I.1.- H.2.- CN.4.s CN.5.s Wb.6.v Wa.6.v "
+    "H.3.- Wa.7.v N.6.- Ea.0.- Ea.1.- D.2.s Wb.7.v D.3.s CN.6.s N.7.- Ba.2.- T.4.- QN.2.- CN.7.s Oa.0.s "
+    "T.5.- I.2.- T.6.- QN.3.- C.4.s C.5.v Oa.1.s Q.4.- C.6.v T.7.- Ea.2.- Bb.1.- Eb.0.- Bb.2.- Eb.1.- "
+    "Ob.0.v H.4.- Oa.2.v Eb.2.- Ob.1.v Bb.3.- I.3.- Ba.3.- Eb.3.- D.4.s Q.5.- I.4.- Bb.4.- Ea.3.- Q.6.- "
+    "Ob.2.s H.5.- C.7.s Ba.4.- Oa.3.s Q.7.- Ob.3.v Eb.4.- D.5.v H.6.- Ea.4.- Bb.5.- Ba.5.- I.5.- Ob.4.v "
+    "D.6.s Eb.5.- H.7.- I.6.- Ba.6.- Oa.4.s D.7.s Ob.5.v Ea.5.- Bb.6.- Oa.5.s Ea.6.- Eb.6.- Ob.6.s Bb.7.- "
+    "I.7.- Oa.6.v Eb.7.- Ob.7.s Ba.7.- Ea.7.- Oa.7.v"
+)
+
+
+def tile_svftrandompatternsingularcoupling_d1p_kernel(
+    tc, x_bytes, x_scale, w0_words, w0_scales, u_words, u_scales, m, pattern, vt_words, vt_scales, out
+):
+    nc = tc.nc
+    with ExitStack() as ctx:
+        keep = ctx.enter_context(tc.tile_pool(name="keep", bufs=1))
+        work = ctx.enter_context(tc.tile_pool(name="work", bufs=8))
+        psum = ctx.enter_context(tc.psum_pool(name="psum", bufs=1))
+
+        xb = keep.tile([P, 8, D], U8, align_bytes=64, name="xb")
+        xs = keep.tile([P, 64], F32, align_bytes=64, name="xs")
+        pat = keep.tile([P, 4, R], BF16, align_bytes=64, name="pat")
+        mt = keep.tile([P, 4, R], BF16, align_bytes=64, name="mt")
+        msk = keep.tile([P, 4, R], BF16, align_bytes=64, name="msk")
+        uw = keep.tile([P, 2, R], U32, align_bytes=64, name="uw")
+        up = keep.tile([P, 2, R], U32, align_bytes=64, name="up")
+        us = keep.tile([P, R], U8, align_bytes=64, name="us")
+        usp = keep.tile([P, R], U8, align_bytes=64, name="usp")
+        vw = keep.tile([P, N], U32, align_bytes=64, name="vw")
+        vs = keep.tile([P, N], U8, align_bytes=64, name="vs")
+        ww = keep.tile([P, 2, N], U32, align_bytes=64, name="ww")
+        ws = keep.tile([P, N], U8, align_bytes=64, name="ws")
+        ident = keep.tile([P, P], F32, align_bytes=64, name="ident")
+        pident = keep.tile([P, P], F32, align_bytes=64, name="pident")
+        msb = keep.tile([P, 2048], BF16, align_bytes=64, name="msb")
+        msq = keep.tile([P, R], U32, align_bytes=64, name="msq")
+        mss = keep.tile([P, R], U8, align_bytes=64, name="mss")
+        nb = keep.tile([P, 4 * N], BF16, align_bytes=64, name="nb")
+        nq = keep.tile([P, N], U32, align_bytes=64, name="nq")
+        nsc = keep.tile([P, N], U8, align_bytes=64, name="nsc")
+        xq = keep.tile([P, 8, 256], U32, align_bytes=64, name="xq")
+        xsc = keep.tile([P, 8, 256], U8, align_bytes=64, name="xsc")
+
+        ctx.enter_context(tc.manual_schedule())
+
+        x_rows = x_bytes.rearrange("(p i) k -> p i k", i=8)
+        m_rows = m.rearrange("(p a) k -> p a k", a=4)
+        p_rows = pattern.rearrange("(p a) k -> p a k", a=4)
+        out_rows = out.rearrange("(p i) n -> p i n", i=8)
+        u_src = u_words.rearrange("g p n t -> p g (n t)").bitcast(I32)
+        w_src = w0_words.rearrange("g p n t -> p g (n t)").bitcast(I32)
+        v_src = vt_words[0].rearrange("p n t -> p (n t)").bitcast(I32)
+
+        def load_x(i, count):
+            nc.sync.dma_start(out=xb[:, i : i + count, :], in_=x_rows[:, i : i + count, :])
+
+        def load_scales(engine, tile, scales, rows):
+            for q in range(4):
+                src = scales[:, 4 * q : 4 * q + 4, :] if rows == 8 else scales[0, 4 * q : 4 * q + 4, :]
+                engine.dma_start(out=tile[32 * q : 32 * q + rows, :].bitcast(I32), in_=src.bitcast(I32))
+
+        warm = keep.tile([P, 16], F32, align_bytes=64, name="warm")
+        warmed = keep.tile([P, 16], F32, align_bytes=64, name="warmed")
+        nc.gpsimd.memset(warm[:], 0.0)
+        nc.scalar.copy(out=warmed[:], in_=warm[:])
+        make_identity(nc, ident[:])
+        nc.gpsimd.tensor_copy(
+            out=pident[:].rearrange("p (t q b) -> p t q b", t=4, q=16),
+            in_=ident[:].rearrange("p (q t b) -> p t q b", q=16, t=4),
+        )
+        nc.vector.memset(us[:].bitcast(I32), 0)
+        nc.vector.memset(vs[:].bitcast(I32), 0)
+        nc.vector.memset(ws[:].bitcast(I32), 0)
+        nc.sync.dma_start(out=xs[:], in_=x_scale.rearrange("(p i) j -> p (i j)", i=8))
+        load_x(0, 1)
+        load_x(1, 1)
+        for a in (0, 2):
+            nc.sync.dma_start(out=pat[:, a : a + 2, :], in_=p_rows[:, a : a + 2, :])
+            nc.sync.dma_start(out=mt[:, a : a + 2, :], in_=m_rows[:, a : a + 2, :])
+        nc.sync.dma_start(out=ww[:, :, 0:512].bitcast(I32), in_=w_src[:, :, 0:512])
+        load_scales(nc.sync, ws, w0_scales, 8)
+        load_x(2, 2)
+        nc.sync.dma_start(out=uw[:].bitcast(I32), in_=u_src)
+        load_scales(nc.sync, us, u_scales, 8)
+        nc.sync.dma_start(out=vw[:].bitcast(I32), in_=v_src)
+        load_scales(nc.sync, vs, vt_scales, 4)
+        nc.sync.dma_start(out=ww[:, :, 512:1024].bitcast(I32), in_=w_src[:, :, 512:1024])
+        load_x(4, 2)
+        load_x(6, 2)
+
+        live = {}
+        turn = {"r": 0, "o": 0}
+
+        def bank(ring):
+            turn[ring] = (turn[ring] + 1) % 4
+            return psum.tile([P, 512], F32, tag="%s%d" % (ring, turn[ring]), name="bank")
+
+        def widen(i, half, eng):
+            if ("xw", i) not in live:
+                live["xw", i] = work.tile([P, D], BF16, align_bytes=64, name="xw")
+            live["split", i, half] = eng == "v"
+            xw = live["xw", i]
+            pairs = xw[:, 512 * half : 512 * half + 512].rearrange("p (u c e) -> p c u e", u=2, e=2)
+            for b in range(4):
+                j = 4 * half + b
+                src = xb[:, i, 128 * j : 128 * j + 128].bitcast(FP8)
+                sc = xs[:, 8 * i + j : 8 * i + j + 1]
+                if eng == "v":
+                    nc.vector.tensor_scalar(
+                        out=pairs[:, 32 * b : 32 * b + 32, :, :],
+                        in0=src.rearrange("p (c u e) -> p c u e", u=2, e=2),
+                        scalar1=sc,
+                        scalar2=None,
+                        op0=ALU.mult,
+                    )
+                else:
+                    nc.scalar.activation(out=xw[:, 128 * j : 128 * j + 128], in_=src, func=ACT.Copy, scale=sc)
+
+        def turn_x(i):
+            tr = bank("r")
+            live["tr", i] = tr
+            words = live["xw", i][:].bitcast(F32)
+            for g in (0, 1):
+                for u in (0, 1):
+                    c = 128 * (2 * g + u)
+                    if live["split", i, g]:
+                        src = words[:, 256 * g + 128 * u : 256 * g + 128 * u + 128]
+                    else:
+                        src = words[:, 256 * g + u : 256 * g + 256 : 2]
+                    nc.tensor.transpose(tr[:, c : c + 128], src, ident[:])
+
+        def copy(eng, dst, src):
+            if eng == "v":
+                nc.vector.tensor_copy(out=dst, in_=src)
+            else:
+                nc.scalar.copy(out=dst, in_=src)
+
+        def copy_x(i, eng):
+            xg = work.tile([P, D], BF16, align_bytes=64, name="xg")
+            live["xg", i] = xg
+            copy(
+                eng,
+                xg[:].bitcast(F32).rearrange("p (g c u) -> p g c u", g=2, u=2),
+                live["tr", i][:].rearrange("p (g u c) -> p g c u", g=2, u=2),
+            )
+
+        def quant_x(i):
+            nc.vector.quantize_mx(out=xq[:, i, :].bitcast(X4), scales=xsc[:, i, :], in_=live["xg", i][:])
+
+        def permute_u():
+            for g in (0, 1):
+                nc.vector.tensor_copy(
+                    out=up[:, g, :].bitcast(I32).rearrange("p (t q j) -> p t q j", t=4, q=16),
+                    in_=uw[:, g, :].bitcast(I32).rearrange("p (q t j) -> p t q j", q=16, t=4),
+                )
+            nc.vector.tensor_copy(
+                out=usp[:].bitcast(I32).rearrange("p (t q j) -> p t q j", t=4, q=16),
+                in_=us[:].bitcast(I32).rearrange("p (q t j) -> p t q j", q=16, t=4),
+            )
+
+        def mask_a(h):
+            a = slice(2 * h, 2 * h + 2)
+            nc.vector.tensor_scalar(out=msk[:, a, :], in0=pat[:, a, :], scalar1=0.25, scalar2=None, op0=ALU.is_lt)
+
+        def mask_b(h):
+            a = slice(2 * h, 2 * h + 2)
+            nc.vector.tensor_tensor(out=msk[:, a, :], in0=msk[:, a, :], in1=mt[:, a, :], op=ALU.mult)
+
+        def turn_m(h):
+            tr = bank("r")
+            live["trm", h] = tr
+            for e in (0, 1):
+                words = msk[:, 2 * h + e, :].bitcast(F32)
+                for u in (0, 1):
+                    c = 128 * (2 * e + u)
+                    nc.tensor.transpose(tr[:, c : c + 128], words[:, u:256:2], pident[:])
+
+        def copy_m(h, eng):
+            dst = msb[:].bitcast(F32).rearrange("p (c a u) -> p c a u", a=4, u=2)[:, :, 2 * h : 2 * h + 2, :]
+            copy(eng, dst, live["trm", h][:].rearrange("p (a u c) -> p c a u", a=2, u=2))
+
+        def quant_m():
+            nc.vector.quantize_mx(out=msq[:].bitcast(X4), scales=mss[:], in_=msb[:])
+
+        def mm_n(c):
+            acc = bank("r")
+            live["n", c] = acc
+            cols = slice(128 * c, 128 * c + 128)
+            for t in range(4):
+                nc.tensor.matmul_mx(
+                    out=acc[:, 128 * t : 128 * t + 128],
+                    lhsT=msq[:, 128 * t : 128 * t + 128].bitcast(X4),
+                    lhsT_scale=mss[:, 128 * t : 128 * t + 128],
+                    rhs=vw[:, cols].bitcast(X4),
+                    rhs_scale=vs[:, cols],
+                    start=True,
+                    stop=True,
+                )
+
+        def copy_n(c, eng):
+            copy(
+                eng,
+                nb[:, 512 * c : 512 * c + 512].rearrange("p (n t) -> p n t", t=4),
+                live["n", c][:].rearrange("p (t n) -> p n t", t=4),
+            )
+
+        def quant_n(h):
+            nc.vector.quantize_mx(
+                out=nq[:, 256 * h : 256 * h + 256].bitcast(X4),
+                scales=nsc[:, 256 * h : 256 * h + 256],
+                in_=nb[:, 1024 * h : 1024 * h + 1024],
+            )
+
+        def mm_h(i):
+            acc = bank("r")
+            live["h", i] = acc
+            for t in range(4):
+                for g in (0, 1):
+                    nc.tensor.matmul_mx(
+                        out=acc[:, 128 * t : 128 * t + 128],
+                        lhsT=up[:, g, 128 * t : 128 * t + 128].bitcast(X4),
+                        lhsT_scale=usp[4 * g : P, 128 * t : 128 * t + 128],
+                        rhs=xq[:, i, 128 * g : 128 * g + 128].bitcast(X4),
+                        rhs_scale=xsc[:, i, 128 * g : 128 * g + 128],
+                        start=(g == 0),
+                        stop=(g == 1),
+                    )
+
+        def copy_h(i, eng):
+            hb = work.tile([P, 512], BF16, align_bytes=64, name="hb")
+            live["hb", i] = hb
+            copy(eng, hb[:].rearrange("p (n t) -> p n t", t=4), live["h", i][:].rearrange("p (t n) -> p n t", t=4))
+
+        def quant_h(i):
+            hq = work.tile([P, P], U32, align_bytes=64, name="hq", bufs=8)
+            hs = work.tile([P, P], U8, align_bytes=64, name="hs", bufs=8)
+            live["hq", i] = (hq, hs)
+            nc.vector.quantize_mx(out=hq[:].bitcast(X4), scales=hs[:], in_=live["hb", i][:])
+
+        def sums(acc, i, cols, part):
+            hq, hs = live["hq", i] if part else (0, 0)
+            for g in (0, 1):
+                if part < 2:
+                    nc.tensor.matmul_mx(
+                        out=acc,
+                        lhsT=xq[:, i, 128 * g : 128 * g + 128].bitcast(X4),
+                        lhsT_scale=xsc[:, i, 128 * g : 128 * g + 128],
+                        rhs=ww[:, g, cols].bitcast(X4),
+                        rhs_scale=ws[4 * g : P, cols],
+                        start=(g == 0),
+                        stop=False,
+                    )
+            if part:
+                nc.tensor.matmul_mx(
+                    out=acc,
+                    lhsT=hq[:].bitcast(X4),
+                    lhsT_scale=hs[:],
+                    rhs=nq[:, cols].bitcast(X4),
+                    rhs_scale=nsc[:, cols],
+                    start=False,
+                    stop=True,
+                )
+
+        def mm_b(i, h):
+            if (i, h) != (7, 0):
+                live["o", i, h] = bank("o")
+                sums(live["o", i, h][:], i, slice(512 * h, 512 * h + 512), 0)
+
+        def mm_d(i, h):
+            if (i, h) != (7, 0):
+                sums(live["o", i, h][:], i, slice(512 * h, 512 * h + 512), 2)
+            else:
+                for k in (0, 1):
+                    acc = bank("o")
+                    live["o", i, h, k] = acc
+                    sums(acc[:, 0:256], i, slice(512 * h + 256 * k, 512 * h + 256 * k + 256), 1)
+
+        def store(i, cols, src):
+            nc.sync.dma_start(out=out_rows[:, i, cols], in_=src)
+
+        def finish(i, h, eng):
+            osb = work.tile([P, 512], F32, align_bytes=64, name="osb", bufs=16)
+            if i < 7:
+                copy(eng, osb[:], live["o", i, h][:])
+                store(i, slice(512 * h, 512 * h + 512), osb[:])
+            elif h != 0:
+                acc = live["o", i, h]
+                copy("s", osb[:, 0:256], acc[:, 0:256])
+                copy("v", osb[:, 256:512], acc[:, 256:512])
+                store(i, slice(512 * h, 512 * h + 512), osb[:])
+            else:
+                for k in (0, 1):
+                    acc = live["o", i, h, k]
+                    copy("s", osb[:, 256 * k : 256 * k + 128], acc[:, 0:128])
+                    copy("v", osb[:, 256 * k + 128 : 256 * k + 256], acc[:, 128:256])
+                    store(i, slice(512 * h + 256 * k, 512 * h + 256 * k + 256), osb[:, 256 * k : 256 * k + 256])
+
+        steps = {
+            "Wa": lambda i, e: widen(i, 0, e),
+            "Wb": lambda i, e: widen(i, 1, e),
+            "T": lambda i, e: turn_x(i),
+            "C": copy_x,
+            "Q": lambda i, e: quant_x(i),
+            "UP": lambda i, e: permute_u(),
+            "Ma": lambda i, e: mask_a(i),
+            "Mb": lambda i, e: mask_b(i),
+            "Tm": lambda i, e: turn_m(i),
+            "Cm": copy_m,
+            "Qm": lambda i, e: quant_m(),
+            "N": lambda i, e: mm_n(i),
+            "CN": copy_n,
+            "QN": lambda i, e: quant_n(i),
+            "H": lambda i, e: mm_h(i),
+            "D": copy_h,
+            "I": lambda i, e: quant_h(i),
+            "Ba": lambda i, e: mm_b(i, 0),
+            "Bb": lambda i, e: mm_b(i, 1),
+            "Ea": lambda i, e: mm_d(i, 0),
+            "Eb": lambda i, e: mm_d(i, 1),
+            "Oa": lambda i, e: finish(i, 0, e),
+            "Ob": lambda i, e: finish(i, 1, e),
+        }
+        for step in ORDER.split(" "):
+            kind, index, engine = step.split(".")
+            steps[kind](int(index), engine)

@@ -17,19 +17,6 @@ X4 = mybir.dt.float8_e4m3fn_x4
 ALU = mybir.AluOpType
 ACT = mybir.ActivationFunctionType
 
-ORDER = (
-    "Wa.0.v Wb.0.s Wa.1.v Wb.1.v Ma.0.- T.0.- C.0.v Ma.1.- Mb.0.- Mb.1.- Q.0.- T.1.- Tm.0.- C.1.s Wb.2.s "
-    "Tm.1.- Cm.0.s Cm.1.s Wa.2.v Q.1.- Wb.3.v Ba.0.- T.2.- C.2.s Wa.3.v T.3.- Qm.0.- C.3.s UP.0.- Ba.1.- "
-    "N.0.- Q.2.- N.1.- N.2.- CN.0.s CN.1.v Q.3.- CN.2.s H.0.- N.3.- H.1.- D.0.s Wa.4.v Wa.5.v N.4.- "
-    "CN.3.s N.5.- QN.0.- QN.1.- I.0.- Wb.4.v D.1.s Wb.5.v Bb.0.- I.1.- H.2.- CN.4.s CN.5.s Wb.6.v Wa.6.v "
-    "H.3.- Wa.7.v N.6.- Ea.0.- Ea.1.- D.2.s Wb.7.v D.3.s CN.6.s N.7.- Ba.2.- T.4.- QN.2.- CN.7.s Oa.0.s "
-    "T.5.- I.2.- T.6.- QN.3.- C.4.s C.5.v Oa.1.s Q.4.- C.6.v T.7.- Ea.2.- Bb.1.- Eb.0.- Bb.2.- Eb.1.- "
-    "Ob.0.v H.4.- Oa.2.v Eb.2.- Ob.1.v Bb.3.- I.3.- Ba.3.- Eb.3.- D.4.s Q.5.- I.4.- Bb.4.- Ea.3.- Q.6.- "
-    "Ob.2.s H.5.- C.7.s Ba.4.- Oa.3.s Q.7.- Ob.3.v Eb.4.- D.5.v H.6.- Ea.4.- Bb.5.- Ba.5.- I.5.- Ob.4.v "
-    "D.6.s Eb.5.- H.7.- I.6.- Ba.6.- Oa.4.s D.7.s Ob.5.v Ea.5.- Bb.6.- Oa.5.s Ea.6.- Eb.6.- Ob.6.s Bb.7.- "
-    "I.7.- Oa.6.v Eb.7.- Ob.7.s Ba.7.- Ea.7.- Oa.7.v"
-)
-
 
 def tile_svftrandompatternsingularcoupling_d1p_kernel(
     tc, x_bytes, x_scale, w0_words, w0_scales, u_words, u_scales, m, pattern, vt_words, vt_scales, out
@@ -37,38 +24,46 @@ def tile_svftrandompatternsingularcoupling_d1p_kernel(
     nc = tc.nc
     with ExitStack() as ctx:
         keep = ctx.enter_context(tc.tile_pool(name="keep", bufs=1))
-        work = ctx.enter_context(tc.tile_pool(name="work", bufs=8))
         psum = ctx.enter_context(tc.psum_pool(name="psum", bufs=1))
 
-        xb = keep.tile([P, 8, D], U8, align_bytes=64, name="xb")
-        xs = keep.tile([P, 64], F32, align_bytes=64, name="xs")
-        pat = keep.tile([P, 4, R], BF16, align_bytes=64, name="pat")
-        mt = keep.tile([P, 4, R], BF16, align_bytes=64, name="mt")
-        msk = keep.tile([P, 4, R], BF16, align_bytes=64, name="msk")
-        uw = keep.tile([P, 2, R], U32, align_bytes=64, name="uw")
-        up = keep.tile([P, 2, R], U32, align_bytes=64, name="up")
-        us = keep.tile([P, R], U8, align_bytes=64, name="us")
-        usp = keep.tile([P, R], U8, align_bytes=64, name="usp")
-        vw = keep.tile([P, N], U32, align_bytes=64, name="vw")
-        vs = keep.tile([P, N], U8, align_bytes=64, name="vs")
-        ww = keep.tile([P, 2, N], U32, align_bytes=64, name="ww")
-        ws = keep.tile([P, N], U8, align_bytes=64, name="ws")
-        ident = keep.tile([P, P], F32, align_bytes=64, name="ident")
-        pident = keep.tile([P, P], F32, align_bytes=64, name="pident")
-        msb = keep.tile([P, 2048], BF16, align_bytes=64, name="msb")
-        msq = keep.tile([P, R], U32, align_bytes=64, name="msq")
-        mss = keep.tile([P, R], U8, align_bytes=64, name="mss")
-        nb = keep.tile([P, 4 * N], BF16, align_bytes=64, name="nb")
-        nq = keep.tile([P, N], U32, align_bytes=64, name="nq")
-        nsc = keep.tile([P, N], U8, align_bytes=64, name="nsc")
-        xq = keep.tile([P, 8, 256], U32, align_bytes=64, name="xq")
-        xsc = keep.tile([P, 8, 256], U8, align_bytes=64, name="xsc")
+        def tile(name, shape, dtype):
+            return keep.tile([P] + shape, dtype, align_bytes=64, name=name)
+
+        xb = tile("xb", [8, D], U8)
+        xs = tile("xs", [64], F32)
+        pat = tile("pat", [4 * R], BF16)
+        mt = [tile("mt%d" % h, [2 * R], BF16) for h in (0, 1)]
+        msk = [tile("msk%d" % h, [2 * R], BF16) for h in (0, 1)]
+        uw = tile("uw", [2, R], U32)
+        up = tile("up", [2, R], U32)
+        us = tile("us", [2, R], U8)
+        usp = tile("usp", [2, R], U8)
+        vw = tile("vw", [N], U32)
+        vs = tile("vs", [1, N], U8)
+        ww = [tile("ww%d" % h, [2, 512], U32) for h in (0, 1)]
+        ws = tile("ws", [2, N], U8)
+        ident = tile("ident", [P], F32)
+        pident = tile("pident", [P], F32)
+        msb = tile("msb", [4 * R], BF16)
+        msq = tile("msq", [R], U32)
+        mss = tile("mss", [R], U8)
+        nb = [tile("nb%d" % c, [512], BF16) for c in range(8)]
+        nq = tile("nq", [N], U32)
+        nsc = tile("nsc", [N], U8)
+        xw = [[tile("xw%d%d" % (i, g), [512], BF16) for g in (0, 1)] for i in range(8)]
+        xg = [tile("xg%d" % i, [D], BF16) for i in range(8)]
+        xq = [tile("xq%d" % i, [256], U32) for i in range(8)]
+        xsc = [tile("xsc%d" % i, [256], U8) for i in range(8)]
+        hb = [tile("hb%d" % i, [512], BF16) for i in range(8)]
+        hq = [tile("hq%d" % i, [P], U32) for i in range(8)]
+        hs = [tile("hs%d" % i, [P], U8) for i in range(8)]
+        osb = [tile("osb%d" % i, [N], F32) for i in range(8)]
 
         ctx.enter_context(tc.manual_schedule())
 
         x_rows = x_bytes.rearrange("(p i) k -> p i k", i=8)
-        m_rows = m.rearrange("(p a) k -> p a k", a=4)
-        p_rows = pattern.rearrange("(p a) k -> p a k", a=4)
+        m_rows = m.rearrange("(p h a) k -> p h (a k)", h=2, a=2)
+        p_rows = pattern.rearrange("(p a) k -> p (a k)", a=4)
         out_rows = out.rearrange("(p i) n -> p i n", i=8)
         u_src = u_words.rearrange("g p n t -> p g (n t)").bitcast(I32)
         w_src = w0_words.rearrange("g p n t -> p g (n t)").bitcast(I32)
@@ -77,55 +72,39 @@ def tile_svftrandompatternsingularcoupling_d1p_kernel(
         def load_x(i, count):
             nc.sync.dma_start(out=xb[:, i : i + count, :], in_=x_rows[:, i : i + count, :])
 
-        def load_scales(engine, tile, scales, rows):
-            for q in range(4):
-                src = scales[:, 4 * q : 4 * q + 4, :] if rows == 8 else scales[0, 4 * q : 4 * q + 4, :]
-                engine.dma_start(out=tile[32 * q : 32 * q + rows, :].bitcast(I32), in_=src.bitcast(I32))
+        def load_scales(plane, first, scales):
+            rows = scales.rearrange("g (q r) n -> r q g n", r=4)
+            for r in range(4):
+                nc.sync.dma_start(out=plane[first + r : P : 32, :, :].bitcast(I32), in_=rows[r].bitcast(I32))
 
-        warm = keep.tile([P, 16], F32, align_bytes=64, name="warm")
-        warmed = keep.tile([P, 16], F32, align_bytes=64, name="warmed")
-        nc.gpsimd.memset(warm[:], 0.0)
-        nc.scalar.copy(out=warmed[:], in_=warm[:])
-        make_identity(nc, ident[:])
-        nc.gpsimd.tensor_copy(
-            out=pident[:].rearrange("p (t q b) -> p t q b", t=4, q=16),
-            in_=ident[:].rearrange("p (q t b) -> p t q b", q=16, t=4),
-        )
-        nc.vector.memset(us[:].bitcast(I32), 0)
-        nc.vector.memset(vs[:].bitcast(I32), 0)
-        nc.vector.memset(ws[:].bitcast(I32), 0)
-        nc.sync.dma_start(out=xs[:], in_=x_scale.rearrange("(p i) j -> p (i j)", i=8))
-        load_x(0, 1)
-        load_x(1, 1)
-        for a in (0, 2):
-            nc.sync.dma_start(out=pat[:, a : a + 2, :], in_=p_rows[:, a : a + 2, :])
-            nc.sync.dma_start(out=mt[:, a : a + 2, :], in_=m_rows[:, a : a + 2, :])
-        nc.sync.dma_start(out=ww[:, :, 0:512].bitcast(I32), in_=w_src[:, :, 0:512])
-        load_scales(nc.sync, ws, w0_scales, 8)
-        load_x(2, 2)
-        nc.sync.dma_start(out=uw[:].bitcast(I32), in_=u_src)
-        load_scales(nc.sync, us, u_scales, 8)
-        nc.sync.dma_start(out=vw[:].bitcast(I32), in_=v_src)
-        load_scales(nc.sync, vs, vt_scales, 4)
-        nc.sync.dma_start(out=ww[:, :, 512:1024].bitcast(I32), in_=w_src[:, :, 512:1024])
-        load_x(4, 2)
-        load_x(6, 2)
+        def load_w(h):
+            nc.sync.dma_start(out=ww[h][:].bitcast(I32), in_=w_src[:, :, 512 * h : 512 * h + 512])
+
+        def load_m(h):
+            nc.sync.dma_start(out=mt[h][:], in_=m_rows[:, h, :])
 
         live = {}
-        turn = {"r": 0, "o": 0}
+        idle = list(range(8))
 
-        def bank(ring):
-            turn[ring] = (turn[ring] + 1) % 4
-            return psum.tile([P, 512], F32, tag="%s%d" % (ring, turn[ring]), name="bank")
+        def take(key):
+            b = idle[0]
+            idle.remove(b)
+            live[key] = (b, psum.tile([P, 512], F32, tag="bank%d" % b, name="bank"))
+            return live[key][1]
 
-        def widen(i, half, eng):
-            if ("xw", i) not in live:
-                live["xw", i] = work.tile([P, D], BF16, align_bytes=64, name="xw")
-            live["split", i, half] = eng == "v"
-            xw = live["xw", i]
-            pairs = xw[:, 512 * half : 512 * half + 512].rearrange("p (u c e) -> p c u e", u=2, e=2)
+        def empty(key, eng, dst, view):
+            b, acc = live[key]
+            if eng == "v":
+                nc.vector.tensor_copy(out=dst, in_=view(acc))
+            else:
+                nc.scalar.copy(out=dst, in_=view(acc))
+            idle.append(b)
+
+        def widen(i, g, eng):
+            live["split", i, g] = eng == "v"
+            pairs = xw[i][g][:].rearrange("p (u c e) -> p c u e", u=2, e=2)
             for b in range(4):
-                j = 4 * half + b
+                j = 4 * g + b
                 src = xb[:, i, 128 * j : 128 * j + 128].bitcast(FP8)
                 sc = xs[:, 8 * i + j : 8 * i + j + 1]
                 if eng == "v":
@@ -137,77 +116,61 @@ def tile_svftrandompatternsingularcoupling_d1p_kernel(
                         op0=ALU.mult,
                     )
                 else:
-                    nc.scalar.activation(out=xw[:, 128 * j : 128 * j + 128], in_=src, func=ACT.Copy, scale=sc)
+                    nc.scalar.activation(out=xw[i][g][:, 128 * b : 128 * b + 128], in_=src, func=ACT.Copy, scale=sc)
 
         def turn_x(i):
-            tr = bank("r")
-            live["tr", i] = tr
-            words = live["xw", i][:].bitcast(F32)
+            tr = take(("tr", i))
             for g in (0, 1):
+                words = xw[i][g][:].bitcast(F32)
                 for u in (0, 1):
                     c = 128 * (2 * g + u)
-                    if live["split", i, g]:
-                        src = words[:, 256 * g + 128 * u : 256 * g + 128 * u + 128]
-                    else:
-                        src = words[:, 256 * g + u : 256 * g + 256 : 2]
+                    src = words[:, 128 * u : 128 * u + 128] if live["split", i, g] else words[:, u:256:2]
                     nc.tensor.transpose(tr[:, c : c + 128], src, ident[:])
 
-        def copy(eng, dst, src):
-            if eng == "v":
-                nc.vector.tensor_copy(out=dst, in_=src)
-            else:
-                nc.scalar.copy(out=dst, in_=src)
-
         def copy_x(i, eng):
-            xg = work.tile([P, D], BF16, align_bytes=64, name="xg")
-            live["xg", i] = xg
-            copy(
-                eng,
-                xg[:].bitcast(F32).rearrange("p (g c u) -> p g c u", g=2, u=2),
-                live["tr", i][:].rearrange("p (g u c) -> p g c u", g=2, u=2),
-            )
+            dst = xg[i][:].bitcast(F32).rearrange("p (g c u) -> p g c u", g=2, u=2)
+            empty(("tr", i), eng, dst, lambda acc: acc[:].rearrange("p (g u c) -> p g c u", g=2, u=2))
 
         def quant_x(i):
-            nc.vector.quantize_mx(out=xq[:, i, :].bitcast(X4), scales=xsc[:, i, :], in_=live["xg", i][:])
+            nc.vector.quantize_mx(out=xq[i][:].bitcast(X4), scales=xsc[i][:], in_=xg[i][:])
 
         def permute_u():
-            for g in (0, 1):
-                nc.vector.tensor_copy(
-                    out=up[:, g, :].bitcast(I32).rearrange("p (t q j) -> p t q j", t=4, q=16),
-                    in_=uw[:, g, :].bitcast(I32).rearrange("p (q t j) -> p t q j", q=16, t=4),
-                )
             nc.vector.tensor_copy(
-                out=usp[:].bitcast(I32).rearrange("p (t q j) -> p t q j", t=4, q=16),
-                in_=us[:].bitcast(I32).rearrange("p (q t j) -> p t q j", q=16, t=4),
+                out=up[:].bitcast(I32).rearrange("p g (t q j) -> p g t q j", t=4, q=16),
+                in_=uw[:].bitcast(I32).rearrange("p g (q t j) -> p g t q j", q=16, t=4),
+            )
+            nc.vector.tensor_copy(
+                out=usp[:].bitcast(I32).rearrange("p g (t q j) -> p g t q j", t=4, q=16),
+                in_=us[:].bitcast(I32).rearrange("p g (q t j) -> p g t q j", q=16, t=4),
             )
 
-        def mask_a(h):
-            a = slice(2 * h, 2 * h + 2)
-            nc.vector.tensor_scalar(out=msk[:, a, :], in0=pat[:, a, :], scalar1=0.25, scalar2=None, op0=ALU.is_lt)
+        def by_word(t):
+            return t.rearrange("p (c u e) -> p u c e", u=2, e=2)
 
-        def mask_b(h):
-            a = slice(2 * h, 2 * h + 2)
-            nc.vector.tensor_tensor(out=msk[:, a, :], in0=msk[:, a, :], in1=mt[:, a, :], op=ALU.mult)
+        def mask_test(h):
+            dst = msk[h][:].rearrange("p (u c e) -> p u c e", u=2, e=2)
+            nc.vector.tensor_scalar(out=dst, in0=by_word(pat[:, 1024 * h : 1024 * h + 1024]), scalar1=0.25, scalar2=None, op0=ALU.is_lt)
+
+        def mask_apply(h):
+            dst = msk[h][:].rearrange("p (u c e) -> p u c e", u=2, e=2)
+            nc.vector.tensor_tensor(out=dst, in0=dst, in1=by_word(mt[h][:]), op=ALU.mult)
 
         def turn_m(h):
-            tr = bank("r")
-            live["trm", h] = tr
-            for e in (0, 1):
-                words = msk[:, 2 * h + e, :].bitcast(F32)
-                for u in (0, 1):
-                    c = 128 * (2 * e + u)
-                    nc.tensor.transpose(tr[:, c : c + 128], words[:, u:256:2], pident[:])
+            tr = take(("trm", h))
+            words = msk[h][:].bitcast(F32)
+            for s in range(4):
+                nc.tensor.transpose(tr[:, 128 * s : 128 * s + 128], words[:, 128 * s : 128 * s + 128], pident[:])
 
         def copy_m(h, eng):
             dst = msb[:].bitcast(F32).rearrange("p (c a u) -> p c a u", a=4, u=2)[:, :, 2 * h : 2 * h + 2, :]
-            copy(eng, dst, live["trm", h][:].rearrange("p (a u c) -> p c a u", a=2, u=2))
+            empty(("trm", h), eng, dst, lambda acc: acc[:].rearrange("p (u a c) -> p c a u", a=2, u=2))
 
-        def quant_m():
-            nc.vector.quantize_mx(out=msq[:].bitcast(X4), scales=mss[:], in_=msb[:])
+        def quant_m(t):
+            cols = slice(128 * t, 128 * t + 128)
+            nc.vector.quantize_mx(out=msq[:, cols].bitcast(X4), scales=mss[:, cols], in_=msb[:, 512 * t : 512 * t + 512])
 
         def mm_n(c):
-            acc = bank("r")
-            live["n", c] = acc
+            acc = take(("n", c))
             cols = slice(128 * c, 128 * c + 128)
             for t in range(4):
                 nc.tensor.matmul_mx(
@@ -215,134 +178,177 @@ def tile_svftrandompatternsingularcoupling_d1p_kernel(
                     lhsT=msq[:, 128 * t : 128 * t + 128].bitcast(X4),
                     lhsT_scale=mss[:, 128 * t : 128 * t + 128],
                     rhs=vw[:, cols].bitcast(X4),
-                    rhs_scale=vs[:, cols],
+                    rhs_scale=vs[8:P, 0, cols],
                     start=True,
                     stop=True,
                 )
 
         def copy_n(c, eng):
-            copy(
-                eng,
-                nb[:, 512 * c : 512 * c + 512].rearrange("p (n t) -> p n t", t=4),
-                live["n", c][:].rearrange("p (t n) -> p n t", t=4),
-            )
+            dst = nb[c][:].rearrange("p (n t) -> p n t", t=4)
+            empty(("n", c), eng, dst, lambda acc: acc[:].rearrange("p (t n) -> p n t", t=4))
 
-        def quant_n(h):
-            nc.vector.quantize_mx(
-                out=nq[:, 256 * h : 256 * h + 256].bitcast(X4),
-                scales=nsc[:, 256 * h : 256 * h + 256],
-                in_=nb[:, 1024 * h : 1024 * h + 1024],
-            )
+        def quant_n(c):
+            cols = slice(128 * c, 128 * c + 128)
+            nc.vector.quantize_mx(out=nq[:, cols].bitcast(X4), scales=nsc[:, cols], in_=nb[c][:])
 
         def mm_h(i):
-            acc = bank("r")
-            live["h", i] = acc
+            acc = take(("h", i))
             for t in range(4):
                 for g in (0, 1):
                     nc.tensor.matmul_mx(
                         out=acc[:, 128 * t : 128 * t + 128],
                         lhsT=up[:, g, 128 * t : 128 * t + 128].bitcast(X4),
-                        lhsT_scale=usp[4 * g : P, 128 * t : 128 * t + 128],
-                        rhs=xq[:, i, 128 * g : 128 * g + 128].bitcast(X4),
-                        rhs_scale=xsc[:, i, 128 * g : 128 * g + 128],
+                        lhsT_scale=usp[4:P, g, 128 * t : 128 * t + 128],
+                        rhs=xq[i][:, 128 * g : 128 * g + 128].bitcast(X4),
+                        rhs_scale=xsc[i][:, 128 * g : 128 * g + 128],
                         start=(g == 0),
                         stop=(g == 1),
                     )
 
         def copy_h(i, eng):
-            hb = work.tile([P, 512], BF16, align_bytes=64, name="hb")
-            live["hb", i] = hb
-            copy(eng, hb[:].rearrange("p (n t) -> p n t", t=4), live["h", i][:].rearrange("p (t n) -> p n t", t=4))
+            dst = hb[i][:].rearrange("p (n t) -> p n t", t=4)
+            empty(("h", i), eng, dst, lambda acc: acc[:].rearrange("p (t n) -> p n t", t=4))
 
         def quant_h(i):
-            hq = work.tile([P, P], U32, align_bytes=64, name="hq", bufs=8)
-            hs = work.tile([P, P], U8, align_bytes=64, name="hs", bufs=8)
-            live["hq", i] = (hq, hs)
-            nc.vector.quantize_mx(out=hq[:].bitcast(X4), scales=hs[:], in_=live["hb", i][:])
+            nc.vector.quantize_mx(out=hq[i][:].bitcast(X4), scales=hs[i][:], in_=hb[i][:])
 
-        def sums(acc, i, cols, part):
-            hq, hs = live["hq", i] if part else (0, 0)
+        def mm_b(i, c0, width=512):
+            acc = take(("o", i, c0))
             for g in (0, 1):
-                if part < 2:
-                    nc.tensor.matmul_mx(
-                        out=acc,
-                        lhsT=xq[:, i, 128 * g : 128 * g + 128].bitcast(X4),
-                        lhsT_scale=xsc[:, i, 128 * g : 128 * g + 128],
-                        rhs=ww[:, g, cols].bitcast(X4),
-                        rhs_scale=ws[4 * g : P, cols],
-                        start=(g == 0),
-                        stop=False,
-                    )
-            if part:
                 nc.tensor.matmul_mx(
-                    out=acc,
-                    lhsT=hq[:].bitcast(X4),
-                    lhsT_scale=hs[:],
-                    rhs=nq[:, cols].bitcast(X4),
-                    rhs_scale=nsc[:, cols],
-                    start=False,
-                    stop=True,
+                    out=acc[:, 0:width],
+                    lhsT=xq[i][:, 128 * g : 128 * g + 128].bitcast(X4),
+                    lhsT_scale=xsc[i][:, 128 * g : 128 * g + 128],
+                    rhs=ww[c0 // 512][:, g, c0 % 512 : c0 % 512 + width].bitcast(X4),
+                    rhs_scale=ws[:, g, c0 : c0 + width],
+                    start=(g == 0),
+                    stop=False,
                 )
 
-        def mm_b(i, h):
-            if (i, h) != (7, 0):
-                live["o", i, h] = bank("o")
-                sums(live["o", i, h][:], i, slice(512 * h, 512 * h + 512), 0)
+        def mm_d(i, c0, width=512):
+            nc.tensor.matmul_mx(
+                out=live["o", i, c0][1][:, 0:width],
+                lhsT=hq[i][:].bitcast(X4),
+                lhsT_scale=hs[i][:],
+                rhs=nq[:, c0 : c0 + width].bitcast(X4),
+                rhs_scale=nsc[:, c0 : c0 + width],
+                start=False,
+                stop=True,
+            )
 
-        def mm_d(i, h):
-            if (i, h) != (7, 0):
-                sums(live["o", i, h][:], i, slice(512 * h, 512 * h + 512), 2)
-            else:
-                for k in (0, 1):
-                    acc = bank("o")
-                    live["o", i, h, k] = acc
-                    sums(acc[:, 0:256], i, slice(512 * h + 256 * k, 512 * h + 256 * k + 256), 1)
+        def finish(i, c0, eng, width=512):
+            cols = slice(c0, c0 + width)
+            empty(("o", i, c0), eng, osb[i][:, cols], lambda acc: acc[:, 0:width])
+            nc.sync.dma_start(out=out_rows[:, i, cols], in_=osb[i][:, cols])
 
-        def store(i, cols, src):
-            nc.sync.dma_start(out=out_rows[:, i, cols], in_=src)
+        nc.vector.memset(ws[:].bitcast(I32), 0)
+        nc.vector.memset(us[:].bitcast(I32), 0)
+        nc.vector.memset(vs[:].bitcast(I32), 0)
+        make_identity(nc, ident[:])
+        nc.scalar.copy(
+            out=pident[:].rearrange("p (t q b) -> p t q b", t=4, q=16),
+            in_=ident[:].rearrange("p (q t b) -> p t q b", q=16, t=4),
+        )
+        nc.sync.dma_start(out=xs[:], in_=x_scale.rearrange("(p i) j -> p (i j)", i=8))
+        load_x(0, 1)
+        load_x(1, 1)
+        load_x(2, 2)
+        load_scales(ws, 0, w0_scales)
+        load_w(0)
+        nc.sync.dma_start(out=uw[:].bitcast(I32), in_=u_src)
+        load_scales(us, 4, u_scales)
+        nc.sync.dma_start(out=pat[:], in_=p_rows)
+        load_m(0)
+        load_m(1)
+        nc.sync.dma_start(out=vw[:].bitcast(I32), in_=v_src)
+        load_scales(vs, 8, vt_scales)
+        load_x(4, 2)
+        load_x(6, 2)
+        load_w(1)
 
-        def finish(i, h, eng):
-            osb = work.tile([P, 512], F32, align_bytes=64, name="osb", bufs=16)
-            if i < 7:
-                copy(eng, osb[:], live["o", i, h][:])
-                store(i, slice(512 * h, 512 * h + 512), osb[:])
-            elif h != 0:
-                acc = live["o", i, h]
-                copy("s", osb[:, 0:256], acc[:, 0:256])
-                copy("v", osb[:, 256:512], acc[:, 256:512])
-                store(i, slice(512 * h, 512 * h + 512), osb[:])
-            else:
-                for k in (0, 1):
-                    acc = live["o", i, h, k]
-                    copy("s", osb[:, 256 * k : 256 * k + 128], acc[:, 0:128])
-                    copy("v", osb[:, 256 * k + 128 : 256 * k + 256], acc[:, 128:256])
-                    store(i, slice(512 * h + 256 * k, 512 * h + 256 * k + 256), osb[:, 256 * k : 256 * k + 256])
-
-        steps = {
-            "Wa": lambda i, e: widen(i, 0, e),
-            "Wb": lambda i, e: widen(i, 1, e),
-            "T": lambda i, e: turn_x(i),
-            "C": copy_x,
-            "Q": lambda i, e: quant_x(i),
-            "UP": lambda i, e: permute_u(),
-            "Ma": lambda i, e: mask_a(i),
-            "Mb": lambda i, e: mask_b(i),
-            "Tm": lambda i, e: turn_m(i),
-            "Cm": copy_m,
-            "Qm": lambda i, e: quant_m(),
-            "N": lambda i, e: mm_n(i),
-            "CN": copy_n,
-            "QN": lambda i, e: quant_n(i),
-            "H": lambda i, e: mm_h(i),
-            "D": copy_h,
-            "I": lambda i, e: quant_h(i),
-            "Ba": lambda i, e: mm_b(i, 0),
-            "Bb": lambda i, e: mm_b(i, 1),
-            "Ea": lambda i, e: mm_d(i, 0),
-            "Eb": lambda i, e: mm_d(i, 1),
-            "Oa": lambda i, e: finish(i, 0, e),
-            "Ob": lambda i, e: finish(i, 1, e),
-        }
-        for step in ORDER.split(" "):
-            kind, index, engine = step.split(".")
-            steps[kind](int(index), engine)
+        widen(0, 0, "v")
+        widen(0, 1, "v")
+        widen(1, 0, "v")
+        widen(1, 1, "s")
+        for i in (2, 3):
+            widen(i, 0, "v")
+            widen(i, 1, "v")
+        for i in range(4):
+            turn_x(i)
+            copy_x(i, "s")
+        for i in range(3):
+            quant_x(i)
+            mm_b(i, 0)
+        permute_u()
+        quant_x(3)
+        for i in range(3):
+            mm_h(i)
+            copy_h(i, "s")
+        for h in (0, 1):
+            mask_test(h)
+        for h in (0, 1):
+            mask_apply(h)
+            turn_m(h)
+        quant_h(0)
+        mm_h(3)
+        mm_b(3, 0)
+        copy_m(0, "v")
+        copy_m(1, "s")
+        copy_h(3, "s")
+        quant_h(1)
+        for t in range(4):
+            quant_m(t)
+        quant_h(2)
+        widen(4, 0, "v")
+        quant_h(3)
+        for c in range(8):
+            mm_n(c)
+            copy_n(c, "v" if c % 3 == 1 else "s")
+            if c > 0:
+                quant_n(c - 1)
+        mm_b(0, 512)
+        for i in range(4):
+            mm_d(i, 0)
+            finish(i, 0, "s")
+        widen(4, 1, "v")
+        quant_n(7)
+        for i in (5, 6, 7):
+            widen(i, 0, "v")
+            widen(i, 1, "v")
+        mm_b(1, 512)
+        for i in range(3):
+            if i == 2:
+                mm_b(i, 512)
+            mm_d(i, 512)
+            finish(i, 512, "s")
+        for i in range(4, 8):
+            turn_x(i)
+            copy_x(i, "v" if i % 2 == 0 else "s")
+            if i > 4:
+                quant_x(i - 1)
+        quant_x(7)
+        mm_b(3, 512)
+        mm_d(3, 512)
+        finish(3, 512, "s")
+        for i in (4, 5):
+            mm_h(i)
+            copy_h(i, "s")
+        quant_h(4)
+        mm_b(4, 512)
+        for i in range(4, 7):
+            mm_b(i, 0)
+            mm_d(i, 0)
+            quant_h(i + 1)
+            finish(i, 0, "v")
+            if i > 4:
+                mm_b(i, 512)
+            mm_d(i, 512)
+            if i < 6:
+                mm_h(i + 2)
+            finish(i, 512, "s")
+            if i < 6:
+                copy_h(i + 2, "s")
+        for c0, width, eng in ((0, 512, "v"), (512, 256, "s"), (768, 256, "v")):
+            mm_b(7, c0, width)
+            mm_d(7, c0, width)
+            finish(7, c0, eng, width)

@@ -100,6 +100,12 @@ def tile_svftrandompatternsingularcoupling_d1p_kernel(
                 nc.scalar.copy(out=dst, in_=view(acc))
             idle.append(b)
 
+        def warm(count):
+            acc = take("warm")
+            for k in range(count):
+                nc.tensor.matmul(acc[:, 0:P], lhsT=ident[:], rhs=ident[:], start=True, stop=True)
+            idle.append(live["warm"][0])
+
         def widen(i, g, eng):
             live["split", i, g] = eng == "v"
             pairs = xw[i][g][:].rearrange("p (u c e) -> p c u e", u=2, e=2)
@@ -266,6 +272,7 @@ def tile_svftrandompatternsingularcoupling_d1p_kernel(
         load_x(6, 2)
         load_w(1)
 
+        warm(3)
         widen(0, 0, "v")
         widen(0, 1, "v")
         widen(1, 0, "v")
@@ -275,6 +282,8 @@ def tile_svftrandompatternsingularcoupling_d1p_kernel(
             widen(i, 1, "v")
         for i in range(4):
             turn_x(i)
+            if i in (0, 2):
+                warm(1)
             copy_x(i, "s")
         for i in range(3):
             quant_x(i)

@@ -34,14 +34,14 @@ def tile_svftrandompatternsingularcoupling_d1p_kernel(
         pat = tile("pat", [4 * R], BF16)
         mt = [tile("mt%d" % h, [2 * R], BF16) for h in (0, 1)]
         msk = [tile("msk%d" % h, [2 * R], BF16) for h in (0, 1)]
-        uw = tile("uw", [2, R], U32)
-        up = tile("up", [2, R], U32)
+        uw = [tile("uw%d" % g, [R], U32) for g in (0, 1)]
+        up = [tile("up%d" % g, [R], U32) for g in (0, 1)]
         us = tile("us", [2, R], U8)
         usp = tile("usp", [2, R], U8)
         vw = tile("vw", [N], U32)
         vs = tile("vs", [1, N], U8)
         ww = [tile("ww%d" % h, [2, 512], U32) for h in (0, 1)]
-        ws = tile("ws", [2, N], U8)
+        ws = [tile("ws%d" % h, [2, 512], U8) for h in (0, 1)]
         ident = tile("ident", [P], F32)
         pident = tile("pident", [P], F32)
         msb = tile("msb", [4 * R], BF16)
@@ -78,6 +78,7 @@ def tile_svftrandompatternsingularcoupling_d1p_kernel(
                 nc.sync.dma_start(out=plane[first + r : P : 32, :, :].bitcast(I32), in_=rows[r].bitcast(I32))
 
         def load_w(h):
+            load_scales(ws[h], 0, w0_scales[:, :, 512 * h : 512 * h + 512])
             nc.sync.dma_start(out=ww[h][:].bitcast(I32), in_=w_src[:, :, 512 * h : 512 * h + 512])
 
         def load_m(h):
@@ -124,9 +125,9 @@ def tile_svftrandompatternsingularcoupling_d1p_kernel(
                 else:
                     nc.scalar.activation(out=xw[i][g][:, 128 * b : 128 * b + 128], in_=src, func=ACT.Copy, scale=sc)
 
-        def turn_x(i):
-            tr = take(("tr", i))
-            for g in (0, 1):
+        def turn_x(i, halves=(0, 1)):
+            tr = take(("tr", i)) if 0 in halves else live["tr", i][1]
+            for g in halves:
                 words = xw[i][g][:].bitcast(F32)
                 for u in (0, 1):
                     c = 128 * (2 * g + u)
@@ -140,11 +141,13 @@ def tile_svftrandompatternsingularcoupling_d1p_kernel(
         def quant_x(i):
             nc.vector.quantize_mx(out=xq[i][:].bitcast(X4), scales=xsc[i][:], in_=xg[i][:])
 
-        def permute_u():
+        def permute_u(g):
             nc.vector.tensor_copy(
-                out=up[:].bitcast(I32).rearrange("p g (t q j) -> p g t q j", t=4, q=16),
-                in_=uw[:].bitcast(I32).rearrange("p g (q t j) -> p g t q j", q=16, t=4),
+                out=up[g][:].bitcast(I32).rearrange("p (t q j) -> p t q j", t=4, q=16),
+                in_=uw[g][:].bitcast(I32).rearrange("p (q t j) -> p t q j", q=16, t=4),
             )
+
+        def permute_u_scales():
             nc.vector.tensor_copy(
                 out=usp[:].bitcast(I32).rearrange("p g (t q j) -> p g t q j", t=4, q=16),
                 in_=us[:].bitcast(I32).rearrange("p g (q t j) -> p g t q j", q=16, t=4),
@@ -199,16 +202,16 @@ def tile_svftrandompatternsingularcoupling_d1p_kernel(
 
         def mm_h(i):
             acc = take(("h", i))
-            for t in range(4):
-                for g in (0, 1):
+            for g in (0, 1):
+                for t in range(4):
                     nc.tensor.matmul_mx(
                         out=acc[:, 128 * t : 128 * t + 128],
-                        lhsT=up[:, g, 128 * t : 128 * t + 128].bitcast(X4),
+                        lhsT=up[g][:, 128 * t : 128 * t + 128].bitcast(X4),
                         lhsT_scale=usp[4:P, g, 128 * t : 128 * t + 128],
                         rhs=xq[i][:, 128 * g : 128 * g + 128].bitcast(X4),
                         rhs_scale=xsc[i][:, 128 * g : 128 * g + 128],
-                        start=(g == 0),
-                        stop=(g == 1),
+                        start=(g == 0 and t == 0),
+                        stop=(g == 1 and t == 3),
                     )
 
         def copy_h(i, eng):
@@ -226,7 +229,7 @@ def tile_svftrandompatternsingularcoupling_d1p_kernel(
                     lhsT=xq[i][:, 128 * g : 128 * g + 128].bitcast(X4),
                     lhsT_scale=xsc[i][:, 128 * g : 128 * g + 128],
                     rhs=ww[c0 // 512][:, g, c0 % 512 : c0 % 512 + width].bitcast(X4),
-                    rhs_scale=ws[:, g, c0 : c0 + width],
+                    rhs_scale=ws[c0 // 512][:, g, c0 % 512 : c0 % 512 + width],
                     start=(g == 0),
                     stop=False,
                 )
@@ -247,9 +250,8 @@ def tile_svftrandompatternsingularcoupling_d1p_kernel(
             empty(("o", i, c0), eng, osb[i][:, cols], lambda acc: acc[:, 0:width])
             nc.sync.dma_start(out=out_rows[:, i, cols], in_=osb[i][:, cols])
 
-        nc.vector.memset(ws[:].bitcast(I32), 0)
-        nc.vector.memset(us[:].bitcast(I32), 0)
-        nc.vector.memset(vs[:].bitcast(I32), 0)
+        for plane in (us, ws[0], vs, ws[1]):
+            nc.vector.memset(plane[:].bitcast(I32), 0)
         make_identity(nc, ident[:])
         nc.scalar.copy(
             out=pident[:].rearrange("p (t q b) -> p t q b", t=4, q=16),
@@ -259,105 +261,107 @@ def tile_svftrandompatternsingularcoupling_d1p_kernel(
         load_x(0, 1)
         load_x(1, 1)
         load_x(2, 2)
-        load_scales(ws, 0, w0_scales)
-        load_w(0)
-        nc.sync.dma_start(out=uw[:].bitcast(I32), in_=u_src)
         load_scales(us, 4, u_scales)
+        for g in (0, 1):
+            nc.sync.dma_start(out=uw[g][:].bitcast(I32), in_=u_src[:, g, :])
+        load_x(4, 1)
         nc.sync.dma_start(out=pat[:], in_=p_rows)
         load_m(0)
         load_m(1)
-        nc.sync.dma_start(out=vw[:].bitcast(I32), in_=v_src)
+        load_w(0)
         load_scales(vs, 8, vt_scales)
-        load_x(4, 2)
-        load_x(6, 2)
+        nc.sync.dma_start(out=vw[:].bitcast(I32), in_=v_src)
+        load_x(5, 3)
         load_w(1)
+
+        def group(i, c0, eng, width=512):
+            mm_b(i, c0, width)
+            mm_d(i, c0, width)
+            finish(i, c0, eng, width)
 
         warm(3)
         widen(0, 0, "v")
         widen(0, 1, "v")
         widen(1, 0, "v")
         widen(1, 1, "s")
-        for i in (2, 3):
-            widen(i, 0, "v")
-            widen(i, 1, "v")
+        widen(2, 0, "v")
+        widen(2, 1, "s")
+        widen(3, 0, "v")
+        widen(3, 1, "v")
         for i in range(4):
             turn_x(i)
-            if i in (0, 2):
+            if i in (1, 3):
                 warm(1)
             copy_x(i, "s")
-        for i in range(3):
-            quant_x(i)
-            mm_b(i, 0)
-        permute_u()
+        permute_u_scales()
+        permute_u(0)
+        quant_x(0)
+        permute_u(1)
+        quant_x(1)
+        widen(4, 0, "v")
+        quant_x(2)
+        mask_test(0)
         quant_x(3)
-        for i in range(3):
+        for i in range(4):
             mm_h(i)
             copy_h(i, "s")
-        for h in (0, 1):
-            mask_test(h)
+        mask_test(1)
+        turn_x(4, (0,))
         for h in (0, 1):
             mask_apply(h)
             turn_m(h)
+        widen(4, 1, "v")
+        turn_x(4, (1,))
         quant_h(0)
-        mm_h(3)
-        mm_b(3, 0)
         copy_m(0, "v")
         copy_m(1, "s")
-        copy_h(3, "s")
+        copy_x(4, "s")
         quant_h(1)
+        quant_h(2)
+        for i in range(3):
+            mm_b(i, 0)
         for t in range(4):
             quant_m(t)
-        quant_h(2)
-        widen(4, 0, "v")
+        quant_x(4)
         quant_h(3)
+        widen(5, 0, "v")
         for c in range(8):
             mm_n(c)
-            copy_n(c, "v" if c % 3 == 1 else "s")
-            if c > 0:
-                quant_n(c - 1)
-        mm_b(0, 512)
+            copy_n(c, "v" if c in (1, 3, 5) else "s")
+            if c == 3:
+                for k in range(4):
+                    quant_n(k)
+        mm_h(4)
+        mm_b(3, 0)
+        copy_h(4, "s")
+        for k in range(4, 8):
+            quant_n(k)
         for i in range(4):
             mm_d(i, 0)
             finish(i, 0, "s")
-        widen(4, 1, "v")
-        quant_n(7)
-        for i in (5, 6, 7):
+        widen(5, 1, "v")
+        quant_h(4)
+        for i in (6, 7):
             widen(i, 0, "v")
             widen(i, 1, "v")
-        mm_b(1, 512)
-        for i in range(3):
-            if i == 2:
-                mm_b(i, 512)
-            mm_d(i, 512)
-            finish(i, 512, "s")
-        for i in range(4, 8):
+        group(0, 512, "s")
+        group(4, 0, "s")
+        for i in (5, 6, 7):
             turn_x(i)
-            copy_x(i, "v" if i % 2 == 0 else "s")
-            if i > 4:
+            copy_x(i, "s" if i == 6 else "v")
+            if i > 5:
                 quant_x(i - 1)
         quant_x(7)
-        mm_b(3, 512)
-        mm_d(3, 512)
-        finish(3, 512, "s")
-        for i in (4, 5):
-            mm_h(i)
-            copy_h(i, "s")
-        quant_h(4)
-        mm_b(4, 512)
-        for i in range(4, 7):
-            mm_b(i, 0)
-            mm_d(i, 0)
-            quant_h(i + 1)
-            finish(i, 0, "v")
-            if i > 4:
-                mm_b(i, 512)
-            mm_d(i, 512)
-            if i < 6:
-                mm_h(i + 2)
-            finish(i, 512, "s")
-            if i < 6:
-                copy_h(i + 2, "s")
-        for c0, width, eng in ((0, 512, "v"), (512, 256, "s"), (768, 256, "v")):
-            mm_b(7, c0, width)
-            mm_d(7, c0, width)
-            finish(7, c0, eng, width)
+        for i in range(1, 5):
+            group(i, 512, "s")
+            if i > 2:
+                quant_h(i + 2)
+            if i > 1:
+                mm_h(i + 3)
+                copy_h(i + 3, "v")
+        group(5, 0, "s")
+        quant_h(7)
+        group(5, 512, "v")
+        for i in (6, 7):
+            for k in range(4):
+                group(i, 256 * k, "v" if k % 2 else "s", 256)

@@ -362,6 +362,8 @@ def tile_svftrandompatternsingularcoupling_d1p_kernel(
         group(5, 0, "s")
         quant_h(7)
         group(5, 512, "v")
-        for i in (6, 7):
-            for k in range(4):
-                group(i, 256 * k, "v" if k % 2 else "s", 256)
+        group(6, 0, "s")
+        group(6, 512, "v")
+        group(7, 0, "s")
+        group(7, 512, "v", 256)
+        group(7, 768, "s", 256)

@@ -101,10 +101,11 @@ def tile_svftrandompatternsingularcoupling_d1p_kernel(
                 nc.scalar.copy(out=dst, in_=view(acc))
             idle.append(b)
 
-        def warm(count):
+        def warm(reps, cols):
             acc = take("warm")
-            for k in range(count):
-                nc.tensor.matmul(acc[:, 0:P], lhsT=ident[:], rhs=ident[:], start=True, stop=True)
+            rhs = ident[:, 0:cols].unsqueeze(1).to_broadcast([P, reps, cols])
+            dst = acc[:, 0 : reps * cols].rearrange("p (a c) -> p a c", a=reps)
+            nc.tensor.matmul(dst, lhsT=ident[:], rhs=rhs, start=True, stop=True)
             idle.append(live["warm"][0])
 
         def widen(i, g, eng):
@@ -279,7 +280,7 @@ def tile_svftrandompatternsingularcoupling_d1p_kernel(
             mm_d(i, c0, width)
             finish(i, c0, eng, width)
 
-        warm(3)
+        warm(3, 128)
         widen(0, 0, "v")
         widen(0, 1, "v")
         widen(1, 0, "v")
@@ -290,8 +291,8 @@ def tile_svftrandompatternsingularcoupling_d1p_kernel(
         widen(3, 1, "v")
         for i in range(4):
             turn_x(i)
-            if i in (1, 3):
-                warm(1)
+            if i < 3:
+                warm(1, 128 if i < 2 else 64)
             copy_x(i, "s")
         permute_u_scales()
         permute_u(0)

@@ -78,7 +78,7 @@ def tile_svftrandompatternsingularcoupling_d1p_kernel(
                 nc.sync.dma_start(out=plane[first + r : P : 32, :, :].bitcast(I32), in_=rows[r].bitcast(I32))
 
         def load_w(h):
-            load_scales(ws[h], 0, w0_scales[:, :, 512 * h : 512 * h + 512])
+            load_scales(ws[h], 12, w0_scales[:, :, 512 * h : 512 * h + 512])
             nc.sync.dma_start(out=ww[h][:].bitcast(I32), in_=w_src[:, :, 512 * h : 512 * h + 512])
 
         def load_m(h):
@@ -93,19 +93,21 @@ def tile_svftrandompatternsingularcoupling_d1p_kernel(
             live[key] = (b, psum.tile([P, 512], F32, tag="bank%d" % b, name="bank"))
             return live[key][1]
 
-        def empty(key, eng, dst, view):
+        def empty(key, eng, dst, view, last=True):
             b, acc = live[key]
             if eng == "v":
                 nc.vector.tensor_copy(out=dst, in_=view(acc))
             else:
                 nc.scalar.copy(out=dst, in_=view(acc))
-            idle.append(b)
+            if last:
+                idle.append(b)
 
-        def warm(reps, cols):
+        def warm(src, reps):
             acc = take("warm")
-            rhs = ident[:, 0:cols].unsqueeze(1).to_broadcast([P, reps, cols])
+            cols = src.shape[1]
+            rhs = src.unsqueeze(1).to_broadcast([P, reps, cols])
             dst = acc[:, 0 : reps * cols].rearrange("p (a c) -> p a c", a=reps)
-            nc.tensor.matmul(dst, lhsT=ident[:], rhs=rhs, start=True, stop=True)
+            nc.tensor.matmul(dst, lhsT=src[:, 0:P], rhs=rhs, start=True, stop=True)
             idle.append(live["warm"][0])
 
         def widen(i, g, eng):
@@ -171,9 +173,10 @@ def tile_svftrandompatternsingularcoupling_d1p_kernel(
             for s in range(4):
                 nc.tensor.transpose(tr[:, 128 * s : 128 * s + 128], words[:, 128 * s : 128 * s + 128], pident[:])
 
-        def copy_m(h, eng):
-            dst = msb[:].bitcast(F32).rearrange("p (c a u) -> p c a u", a=4, u=2)[:, :, 2 * h : 2 * h + 2, :]
-            empty(("trm", h), eng, dst, lambda acc: acc[:].rearrange("p (u a c) -> p c a u", a=2, u=2))
+        def copy_m(h, eng, c0=0, c1=P):
+            dst = msb[:].bitcast(F32).rearrange("p (c a u) -> p c a u", a=4, u=2)[:, c0:c1, 2 * h : 2 * h + 2, :]
+            view = lambda acc: acc[:].rearrange("p (u a c) -> p c a u", a=2, u=2)[:, c0:c1]
+            empty(("trm", h), eng, dst, view, c1 == P)
 
         def quant_m(t):
             cols = slice(128 * t, 128 * t + 128)
@@ -199,7 +202,7 @@ def tile_svftrandompatternsingularcoupling_d1p_kernel(
 
         def quant_n(c):
             cols = slice(128 * c, 128 * c + 128)
-            nc.vector.quantize_mx(out=nq[:, cols].bitcast(X4), scales=nsc[:, cols], in_=nb[c][:])
+            nc.vector.quantize_mx(out=nq[:, cols].bitcast(X4), scales=nsc[4:P, cols], in_=nb[c][:])
 
         def mm_h(i):
             acc = take(("h", i))
@@ -230,7 +233,7 @@ def tile_svftrandompatternsingularcoupling_d1p_kernel(
                     lhsT=xq[i][:, 128 * g : 128 * g + 128].bitcast(X4),
                     lhsT_scale=xsc[i][:, 128 * g : 128 * g + 128],
                     rhs=ww[c0 // 512][:, g, c0 % 512 : c0 % 512 + width].bitcast(X4),
-                    rhs_scale=ws[c0 // 512][:, g, c0 % 512 : c0 % 512 + width],
+                    rhs_scale=ws[c0 // 512][12:P, g, c0 % 512 : c0 % 512 + width],
                     start=(g == 0),
                     stop=False,
                 )
@@ -241,7 +244,7 @@ def tile_svftrandompatternsingularcoupling_d1p_kernel(
                 lhsT=hq[i][:].bitcast(X4),
                 lhsT_scale=hs[i][:],
                 rhs=nq[:, c0 : c0 + width].bitcast(X4),
-                rhs_scale=nsc[:, c0 : c0 + width],
+                rhs_scale=nsc[4:P, c0 : c0 + width],
                 start=False,
                 stop=True,
             )
@@ -280,7 +283,7 @@ def tile_svftrandompatternsingularcoupling_d1p_kernel(
             mm_d(i, c0, width)
             finish(i, c0, eng, width)
 
-        warm(3, 128)
+        warm(ident[:], 3)
         widen(0, 0, "v")
         widen(0, 1, "v")
         widen(1, 0, "v")
@@ -291,8 +294,7 @@ def tile_svftrandompatternsingularcoupling_d1p_kernel(
         widen(3, 1, "v")
         for i in range(4):
             turn_x(i)
-            if i < 3:
-                warm(1, 128 if i < 2 else 64)
+            warm(ident[:].bitcast(BF16), 1 + i % 2)
             copy_x(i, "s")
         permute_u_scales()
         permute_u(0)

@@ -250,9 +250,10 @@ def tile_svftrandompatternsingularcoupling_d1p_kernel(
             )
 
         def finish(i, c0, eng, width=512):
-            cols = slice(c0, c0 + width)
-            empty(("o", i, c0), eng, osb[i][:, cols], lambda acc: acc[:, 0:width])
-            nc.sync.dma_start(out=out_rows[:, i, cols], in_=osb[i][:, cols])
+            empty(("o", i, c0), eng, osb[i][:, c0 : c0 + width], lambda acc: acc[:, 0:width])
+            if (c0 + width) % 512 == 0:
+                cols = slice(c0 + width - 512, c0 + width)
+                nc.sync.dma_start(out=out_rows[:, i, cols], in_=osb[i][:, cols])
 
         for plane in (us, ws[0], vs, ws[1]):
             nc.vector.memset(plane[:].bitcast(I32), 0)
@@ -365,8 +366,6 @@ def tile_svftrandompatternsingularcoupling_d1p_kernel(
         group(5, 0, "s")
         quant_h(7)
         group(5, 512, "v")
-        group(6, 0, "s")
-        group(6, 512, "v")
-        group(7, 0, "s")
-        group(7, 512, "v", 256)
-        group(7, 768, "s", 256)
+        for i in (6, 7):
+            for k in range(4):
+                group(i, 256 * k, "v" if k % 2 else "s", 256)

@@ -302,7 +302,7 @@ def tile_svftrandompatternsingularcoupling_d1p_kernel(
         quant_x(0)
         permute_u(1)
         quant_x(1)
-        widen(4, 0, "v")
+        widen(4, 0, "s")
         quant_x(2)
         mask_test(0)
         quant_x(3)
@@ -317,15 +317,16 @@ def tile_svftrandompatternsingularcoupling_d1p_kernel(
         widen(4, 1, "v")
         turn_x(4, (1,))
         quant_h(0)
-        copy_m(0, "v")
-        copy_m(1, "s")
-        copy_x(4, "s")
+        copy_m(0, "s")
         quant_h(1)
-        quant_h(2)
+        copy_m(1, "v", 0, 64)
+        copy_m(1, "v", 64, P)
+        copy_x(4, "s")
         for i in range(3):
             mm_b(i, 0)
         for t in range(4):
             quant_m(t)
+        quant_h(2)
         quant_x(4)
         quant_h(3)
         widen(5, 0, "v")

@@ -72,13 +72,15 @@ def tile_svftrandompatternsingularcoupling_d1p_kernel(
         def load_x(i, count):
             nc.sync.dma_start(out=xb[:, i : i + count, :], in_=x_rows[:, i : i + count, :])
 
-        def load_scales(plane, first, scales):
+        def load_scales(plane, first, scales, which=range(4)):
             rows = scales.rearrange("g (q r) n -> r q g n", r=4)
-            for r in range(4):
+            for r in which:
                 nc.sync.dma_start(out=plane[first + r : P : 32, :, :].bitcast(I32), in_=rows[r].bitcast(I32))
 
-        def load_w(h):
+        def load_ws(h):
             load_scales(ws[h], 12, w0_scales[:, :, 512 * h : 512 * h + 512])
+
+        def load_w(h):
             nc.sync.dma_start(out=ww[h][:].bitcast(I32), in_=w_src[:, :, 512 * h : 512 * h + 512])
 
         def load_m(h):
@@ -266,17 +268,19 @@ def tile_svftrandompatternsingularcoupling_d1p_kernel(
         load_x(0, 1)
         load_x(1, 1)
         load_x(2, 2)
+        nc.sync.dma_start(out=uw[0][:].bitcast(I32), in_=u_src[:, 0, :])
         load_scales(us, 4, u_scales)
-        for g in (0, 1):
-            nc.sync.dma_start(out=uw[g][:].bitcast(I32), in_=u_src[:, g, :])
+        nc.sync.dma_start(out=uw[1][:].bitcast(I32), in_=u_src[:, 1, :])
         load_x(4, 1)
         nc.sync.dma_start(out=pat[:], in_=p_rows)
         load_m(0)
         load_m(1)
+        load_ws(0)
         load_w(0)
         load_scales(vs, 8, vt_scales)
         nc.sync.dma_start(out=vw[:].bitcast(I32), in_=v_src)
         load_x(5, 3)
+        load_ws(1)
         load_w(1)
 
         def group(i, c0, eng, width=512):
@@ -297,8 +301,8 @@ def tile_svftrandompatternsingularcoupling_d1p_kernel(
             turn_x(i)
             warm(ident[:].bitcast(BF16), 1 + i % 2)
             copy_x(i, "s")
-        permute_u_scales()
         permute_u(0)
+        permute_u_scales()
         quant_x(0)
         permute_u(1)
         quant_x(1)

@@ -27,7 +27,10 @@ def tile_svftrandompatternsingularcoupling_d1p_kernel(
         psum = ctx.enter_context(tc.psum_pool(name="psum", bufs=1))
 
         def tile(name, shape, dtype):
-            return keep.tile([P] + shape, dtype, align_bytes=64, name=name)
+            return keep.tile([P] + shape, dtype, align_bytes=256, name=name)
+
+        def shifted(name, words):
+            return tile(name, [16 + words], U32)[:, 16:]
 
         xb = tile("xb", [8, D], U8)
         xs = tile("xs", [64], F32)
@@ -35,12 +38,12 @@ def tile_svftrandompatternsingularcoupling_d1p_kernel(
         mt = [tile("mt%d" % h, [2 * R], BF16) for h in (0, 1)]
         msk = [tile("msk%d" % h, [2 * R], BF16) for h in (0, 1)]
         uw = [tile("uw%d" % g, [R], U32) for g in (0, 1)]
-        up = [tile("up%d" % g, [R], U32) for g in (0, 1)]
+        up = [shifted("up%d" % g, R) for g in (0, 1)]
         us = tile("us", [2, R], U8)
         usp = tile("usp", [2, R], U8)
-        vw = tile("vw", [N], U32)
+        vw = shifted("vw", N)
         vs = tile("vs", [1, N], U8)
-        ww = [tile("ww%d" % h, [2, 512], U32) for h in (0, 1)]
+        ww = [shifted("ww%d" % h, 1024).rearrange("p (g n) -> p g n", g=2) for h in (0, 1)]
         ws = [tile("ws%d" % h, [2, 512], U8) for h in (0, 1)]
         ident = tile("ident", [P], F32)
         pident = tile("pident", [P], F32)
@@ -48,7 +51,7 @@ def tile_svftrandompatternsingularcoupling_d1p_kernel(
         msq = tile("msq", [R], U32)
         mss = tile("mss", [R], U8)
         nb = [tile("nb%d" % c, [512], BF16) for c in range(8)]
-        nq = tile("nq", [N], U32)
+        nq = shifted("nq", N)
         nsc = tile("nsc", [N], U8)
         xw = [[tile("xw%d%d" % (i, g), [512], BF16) for g in (0, 1)] for i in range(8)]
         xg = [tile("xg%d" % i, [D], BF16) for i in range(8)]
@@ -72,19 +75,14 @@ def tile_svftrandompatternsingularcoupling_d1p_kernel(
         def load_x(i, count):
             nc.sync.dma_start(out=xb[:, i : i + count, :], in_=x_rows[:, i : i + count, :])
 
-        def load_scales(plane, first, scales, which=range(4)):
+        def load_scales(plane, first, scales):
             rows = scales.rearrange("g (q r) n -> r q g n", r=4)
-            for r in which:
+            for r in range(4):
                 nc.sync.dma_start(out=plane[first + r : P : 32, :, :].bitcast(I32), in_=rows[r].bitcast(I32))
 
-        def load_ws(h):
-            load_scales(ws[h], 12, w0_scales[:, :, 512 * h : 512 * h + 512])
-
         def load_w(h):
+            load_scales(ws[h], 12, w0_scales[:, :, 512 * h : 512 * h + 512])
             nc.sync.dma_start(out=ww[h][:].bitcast(I32), in_=w_src[:, :, 512 * h : 512 * h + 512])
-
-        def load_m(h):
-            nc.sync.dma_start(out=mt[h][:], in_=m_rows[:, h, :])
 
         live = {}
         idle = list(range(8))
@@ -94,6 +92,9 @@ def tile_svftrandompatternsingularcoupling_d1p_kernel(
             idle.remove(b)
             live[key] = (b, psum.tile([P, 512], F32, tag="bank%d" % b, name="bank"))
             return live[key][1]
+
+        def bank(key):
+            return live[key][1] if key in live else take(key)
 
         def empty(key, eng, dst, view, last=True):
             b, acc = live[key]
@@ -112,8 +113,18 @@ def tile_svftrandompatternsingularcoupling_d1p_kernel(
             nc.tensor.matmul(dst, lhsT=src[:, 0:P], rhs=rhs, start=True, stop=True)
             idle.append(live["warm"][0])
 
+        def mx(acc, lhs, rhs, start, stop):
+            nc.tensor.matmul_mx(
+                out=acc, lhsT=lhs[0].bitcast(X4), lhsT_scale=lhs[1], rhs=rhs[0].bitcast(X4), rhs_scale=rhs[1], start=start, stop=stop
+            )
+
+        def x_operand(i, g):
+            return xq[i][:, 128 * g : 128 * g + 128], xsc[i][:, 128 * g : 128 * g + 128]
+
+        widened_by = {}
+
         def widen(i, g, eng):
-            live["split", i, g] = eng == "v"
+            widened_by[i, g] = eng
             pairs = xw[i][g][:].rearrange("p (u c e) -> p c u e", u=2, e=2)
             for b in range(4):
                 j = 4 * g + b
@@ -131,20 +142,21 @@ def tile_svftrandompatternsingularcoupling_d1p_kernel(
                     nc.scalar.activation(out=xw[i][g][:, 128 * b : 128 * b + 128], in_=src, func=ACT.Copy, scale=sc)
 
         def turn_x(i, halves=(0, 1)):
-            tr = take(("tr", i)) if 0 in halves else live["tr", i][1]
+            tr = bank(("tr", i))
             for g in halves:
                 words = xw[i][g][:].bitcast(F32)
                 for u in (0, 1):
                     c = 128 * (2 * g + u)
-                    src = words[:, 128 * u : 128 * u + 128] if live["split", i, g] else words[:, u:256:2]
+                    src = words[:, 128 * u : 128 * u + 128] if widened_by[i, g] == "v" else words[:, u:256:2]
                     nc.tensor.transpose(tr[:, c : c + 128], src, ident[:])
 
         def copy_x(i, eng):
             dst = xg[i][:].bitcast(F32).rearrange("p (g c u) -> p g c u", g=2, u=2)
             empty(("tr", i), eng, dst, lambda acc: acc[:].rearrange("p (g u c) -> p g c u", g=2, u=2))
 
-        def quant_x(i):
-            nc.vector.quantize_mx(out=xq[i][:].bitcast(X4), scales=xsc[i][:], in_=xg[i][:])
+        def quant_x(i, g0=0, g1=2):
+            words = slice(128 * g0, 128 * g1)
+            nc.vector.quantize_mx(out=xq[i][:, words].bitcast(X4), scales=xsc[i][:, words], in_=xg[i][:, 512 * g0 : 512 * g1])
 
         def permute_u(g):
             nc.vector.tensor_copy(
@@ -184,19 +196,12 @@ def tile_svftrandompatternsingularcoupling_d1p_kernel(
             cols = slice(128 * t, 128 * t + 128)
             nc.vector.quantize_mx(out=msq[:, cols].bitcast(X4), scales=mss[:, cols], in_=msb[:, 512 * t : 512 * t + 512])
 
-        def mm_n(c):
-            acc = take(("n", c))
-            cols = slice(128 * c, 128 * c + 128)
-            for t in range(4):
-                nc.tensor.matmul_mx(
-                    out=acc[:, 128 * t : 128 * t + 128],
-                    lhsT=msq[:, 128 * t : 128 * t + 128].bitcast(X4),
-                    lhsT_scale=mss[:, 128 * t : 128 * t + 128],
-                    rhs=vw[:, cols].bitcast(X4),
-                    rhs_scale=vs[8:P, 0, cols],
-                    start=True,
-                    stop=True,
-                )
+        def mm_n(slices, blocks):
+            for t in slices:
+                rows = slice(128 * t, 128 * t + 128)
+                for c in blocks:
+                    cols = slice(128 * c, 128 * c + 128)
+                    mx(bank(("n", c))[:, rows], (msq[:, rows], mss[:, rows]), (vw[:, cols], vs[8:P, 0, cols]), True, True)
 
         def copy_n(c, eng):
             dst = nb[c][:].rearrange("p (n t) -> p n t", t=4)
@@ -206,19 +211,13 @@ def tile_svftrandompatternsingularcoupling_d1p_kernel(
             cols = slice(128 * c, 128 * c + 128)
             nc.vector.quantize_mx(out=nq[:, cols].bitcast(X4), scales=nsc[4:P, cols], in_=nb[c][:])
 
-        def mm_h(i):
-            acc = take(("h", i))
-            for g in (0, 1):
-                for t in range(4):
-                    nc.tensor.matmul_mx(
-                        out=acc[:, 128 * t : 128 * t + 128],
-                        lhsT=up[g][:, 128 * t : 128 * t + 128].bitcast(X4),
-                        lhsT_scale=usp[4:P, g, 128 * t : 128 * t + 128],
-                        rhs=xq[i][:, 128 * g : 128 * g + 128].bitcast(X4),
-                        rhs_scale=xsc[i][:, 128 * g : 128 * g + 128],
-                        start=(g == 0 and t == 0),
-                        stop=(g == 1 and t == 3),
-                    )
+        def mm_h(g, tiles):
+            opened = [("h", i) in live for i in tiles]
+            for t in range(4):
+                rows = slice(128 * t, 128 * t + 128)
+                for i, second in zip(tiles, opened):
+                    first_pass, last_pass = not second and t == 0, second and t == 3
+                    mx(bank(("h", i))[:, rows], (up[g][:, rows], usp[4:P, g, rows]), x_operand(i, g), first_pass, last_pass)
 
         def copy_h(i, eng):
             dst = hb[i][:].rearrange("p (n t) -> p n t", t=4)
@@ -227,35 +226,27 @@ def tile_svftrandompatternsingularcoupling_d1p_kernel(
         def quant_h(i):
             nc.vector.quantize_mx(out=hq[i][:].bitcast(X4), scales=hs[i][:], in_=hb[i][:])
 
-        def mm_b(i, c0, width=512):
-            acc = take(("o", i, c0))
-            for g in (0, 1):
-                nc.tensor.matmul_mx(
-                    out=acc[:, 0:width],
-                    lhsT=xq[i][:, 128 * g : 128 * g + 128].bitcast(X4),
-                    lhsT_scale=xsc[i][:, 128 * g : 128 * g + 128],
-                    rhs=ww[c0 // 512][:, g, c0 % 512 : c0 % 512 + width].bitcast(X4),
-                    rhs_scale=ws[c0 // 512][12:P, g, c0 % 512 : c0 % 512 + width],
-                    start=(g == 0),
-                    stop=False,
-                )
+        def mm_b(i, starts, width=512, halves=(0, 1)):
+            for g in halves:
+                for c0 in starts:
+                    half, cols = c0 // 512, slice(c0 % 512, c0 % 512 + width)
+                    mx(bank(("o", i, c0))[:, 0:width], x_operand(i, g), (ww[half][:, g, cols], ws[half][12:P, g, cols]), g == 0, False)
 
-        def mm_d(i, c0, width=512):
-            nc.tensor.matmul_mx(
-                out=live["o", i, c0][1][:, 0:width],
-                lhsT=hq[i][:].bitcast(X4),
-                lhsT_scale=hs[i][:],
-                rhs=nq[:, c0 : c0 + width].bitcast(X4),
-                rhs_scale=nsc[4:P, c0 : c0 + width],
-                start=False,
-                stop=True,
-            )
+        def mm_d(i, starts, width=512):
+            for c0 in starts:
+                cols = slice(c0, c0 + width)
+                mx(bank(("o", i, c0))[:, 0:width], (hq[i][:], hs[i][:]), (nq[:, cols], nsc[4:P, cols]), False, True)
 
         def finish(i, c0, eng, width=512):
             empty(("o", i, c0), eng, osb[i][:, c0 : c0 + width], lambda acc: acc[:, 0:width])
             if (c0 + width) % 512 == 0:
                 cols = slice(c0 + width - 512, c0 + width)
                 nc.sync.dma_start(out=out_rows[:, i, cols], in_=osb[i][:, cols])
+
+        def group(i, c0, eng):
+            mm_b(i, (c0,))
+            mm_d(i, (c0,))
+            finish(i, c0, eng)
 
         for plane in (us, ws[0], vs, ws[1]):
             nc.vector.memset(plane[:].bitcast(I32), 0)
@@ -273,30 +264,22 @@ def tile_svftrandompatternsingularcoupling_d1p_kernel(
         nc.sync.dma_start(out=uw[1][:].bitcast(I32), in_=u_src[:, 1, :])
         load_x(4, 1)
         nc.sync.dma_start(out=pat[:], in_=p_rows)
-        load_m(0)
-        load_m(1)
-        load_ws(0)
+        for h in (0, 1):
+            nc.sync.dma_start(out=mt[h][:], in_=m_rows[:, h, :])
         load_w(0)
         load_scales(vs, 8, vt_scales)
         nc.sync.dma_start(out=vw[:].bitcast(I32), in_=v_src)
         load_x(5, 3)
-        load_ws(1)
         load_w(1)
 
-        def group(i, c0, eng, width=512):
-            mm_b(i, c0, width)
-            mm_d(i, c0, width)
-            finish(i, c0, eng, width)
+        def h_tile(i):
+            for g in (0, 1):
+                mm_h(g, (i,))
 
         warm(ident[:], 3)
-        widen(0, 0, "v")
-        widen(0, 1, "v")
-        widen(1, 0, "v")
-        widen(1, 1, "s")
-        widen(2, 0, "v")
-        widen(2, 1, "s")
-        widen(3, 0, "v")
-        widen(3, 1, "v")
+        for i in range(4):
+            widen(i, 0, "v")
+            widen(i, 1, "s" if i in (1, 2) else "v")
         for i in range(4):
             turn_x(i)
             warm(ident[:].bitcast(BF16), 1 + i % 2)
@@ -311,7 +294,7 @@ def tile_svftrandompatternsingularcoupling_d1p_kernel(
         mask_test(0)
         quant_x(3)
         for i in range(4):
-            mm_h(i)
+            h_tile(i)
             copy_h(i, "s")
         mask_test(1)
         turn_x(4, (0,))
@@ -327,7 +310,7 @@ def tile_svftrandompatternsingularcoupling_d1p_kernel(
         copy_m(1, "v", 64, P)
         copy_x(4, "s")
         for i in range(3):
-            mm_b(i, 0)
+            mm_b(i, (0,))
         for t in range(4):
             quant_m(t)
         quant_h(2)
@@ -335,18 +318,18 @@ def tile_svftrandompatternsingularcoupling_d1p_kernel(
         quant_h(3)
         widen(5, 0, "v")
         for c in range(8):
-            mm_n(c)
+            mm_n(range(4), (c,))
             copy_n(c, "v" if c in (1, 3, 5) else "s")
             if c == 3:
                 for k in range(4):
                     quant_n(k)
-        mm_h(4)
-        mm_b(3, 0)
+        h_tile(4)
+        mm_b(3, (0,))
         copy_h(4, "s")
         for k in range(4, 8):
             quant_n(k)
         for i in range(4):
-            mm_d(i, 0)
+            mm_d(i, (0,))
             finish(i, 0, "s")
         widen(5, 1, "v")
         quant_h(4)
@@ -366,11 +349,13 @@ def tile_svftrandompatternsingularcoupling_d1p_kernel(
             if i > 2:
                 quant_h(i + 2)
             if i > 1:
-                mm_h(i + 3)
+                h_tile(i + 3)
                 copy_h(i + 3, "v")
         group(5, 0, "s")
         quant_h(7)
         group(5, 512, "v")
         for i in (6, 7):
             for k in range(4):
-                group(i, 256 * k, "v" if k % 2 else "s", 256)
+                mm_b(i, (256 * k,), 256)
+                mm_d(i, (256 * k,), 256)
+                finish(i, 256 * k, "v" if k % 2 else "s", 256)

@@ -282,7 +282,7 @@ def tile_svftrandompatternsingularcoupling_d1p_kernel(
             widen(i, 1, "s" if i in (1, 2) else "v")
         for i in range(4):
             turn_x(i)
-            warm(ident[:].bitcast(BF16), 1 + i % 2)
+            warm(ident[:].bitcast(BF16), 2 - i // 2)
             copy_x(i, "s")
         permute_u(0)
         permute_u_scales()

@@ -158,10 +158,10 @@ def tile_svftrandompatternsingularcoupling_d1p_kernel(
             words = slice(128 * g0, 128 * g1)
             nc.vector.quantize_mx(out=xq[i][:, words].bitcast(X4), scales=xsc[i][:, words], in_=xg[i][:, 512 * g0 : 512 * g1])
 
-        def permute_u(g):
+        def permute_u(g, t0=0, t1=4):
             nc.vector.tensor_copy(
-                out=up[g][:].bitcast(I32).rearrange("p (t q j) -> p t q j", t=4, q=16),
-                in_=uw[g][:].bitcast(I32).rearrange("p (q t j) -> p t q j", q=16, t=4),
+                out=up[g][:].bitcast(I32).rearrange("p (t q j) -> p t q j", t=4, q=16)[:, t0:t1],
+                in_=uw[g][:].bitcast(I32).rearrange("p (q t j) -> p t q j", q=16, t=4)[:, t0:t1],
             )
 
         def permute_u_scales():
@@ -248,8 +248,9 @@ def tile_svftrandompatternsingularcoupling_d1p_kernel(
             mm_d(i, (c0,))
             finish(i, c0, eng)
 
-        for plane in (us, ws[0], vs, ws[1]):
+        for plane in (us, vs, ws[0], ws[1]):
             nc.vector.memset(plane[:].bitcast(I32), 0)
+        warm(vs[:, 0, :].bitcast(F32), 2)
         make_identity(nc, ident[:])
         nc.scalar.copy(
             out=pident[:].rearrange("p (t q b) -> p t q b", t=4, q=16),
@@ -267,8 +268,8 @@ def tile_svftrandompatternsingularcoupling_d1p_kernel(
         for h in (0, 1):
             nc.sync.dma_start(out=mt[h][:], in_=m_rows[:, h, :])
         load_w(0)
-        load_scales(vs, 8, vt_scales)
         nc.sync.dma_start(out=vw[:].bitcast(I32), in_=v_src)
+        load_scales(vs, 8, vt_scales)
         load_x(5, 3)
         load_w(1)
 
@@ -276,7 +277,6 @@ def tile_svftrandompatternsingularcoupling_d1p_kernel(
             for g in (0, 1):
                 mm_h(g, (i,))
 
-        warm(ident[:], 3)
         for i in range(4):
             widen(i, 0, "v")
             widen(i, 1, "s" if i in (1, 2) else "v")
@@ -286,9 +286,12 @@ def tile_svftrandompatternsingularcoupling_d1p_kernel(
             copy_x(i, "s")
         permute_u(0)
         permute_u_scales()
-        quant_x(0)
-        permute_u(1)
-        quant_x(1)
+        quant_x(0, 0, 1)
+        quant_x(0, 1, 2)
+        permute_u(1, 0, 2)
+        permute_u(1, 2, 4)
+        quant_x(1, 0, 1)
+        quant_x(1, 1, 2)
         widen(4, 0, "s")
         quant_x(2)
         mask_test(0)

@@ -34,7 +34,7 @@ def tile_svftrandompatternsingularcoupling_d1p_kernel(
 
         xb = tile("xb", [8, D], U8)
         xs = tile("xs", [64], F32)
-        pat = tile("pat", [4 * R], BF16)
+        pat = [tile("pat%d" % h, [2 * R], BF16) for h in (0, 1)]
         mt = [tile("mt%d" % h, [2 * R], BF16) for h in (0, 1)]
         msk = [tile("msk%d" % h, [2 * R], BF16) for h in (0, 1)]
         uw = [tile("uw%d" % g, [R], U32) for g in (0, 1)]
@@ -47,7 +47,7 @@ def tile_svftrandompatternsingularcoupling_d1p_kernel(
         ws = [tile("ws%d" % h, [2, 512], U8) for h in (0, 1)]
         ident = tile("ident", [P], F32)
         pident = tile("pident", [P], F32)
-        msb = tile("msb", [4 * R], BF16)
+        msb = [tile("msb%d" % t, [R], BF16) for t in range(4)]
         msq = tile("msq", [R], U32)
         mss = tile("mss", [R], U8)
         nb = [tile("nb%d" % c, [512], BF16) for c in range(8)]
@@ -65,8 +65,8 @@ def tile_svftrandompatternsingularcoupling_d1p_kernel(
         ctx.enter_context(tc.manual_schedule())
 
         x_rows = x_bytes.rearrange("(p i) k -> p i k", i=8)
-        m_rows = m.rearrange("(p h a) k -> p h (a k)", h=2, a=2)
-        p_rows = pattern.rearrange("(p a) k -> p (a k)", a=4)
+        m_rows = m.rearrange("(q h j a) k -> h q j (a k)", h=2, j=8, a=2)
+        p_rows = pattern.rearrange("(q h j a) k -> h q j (a k)", h=2, j=8, a=2)
         out_rows = out.rearrange("(p i) n -> p i n", i=8)
         u_src = u_words.rearrange("g p n t -> p g (n t)").bitcast(I32)
         w_src = w0_words.rearrange("g p n t -> p g (n t)").bitcast(I32)
@@ -150,9 +150,9 @@ def tile_svftrandompatternsingularcoupling_d1p_kernel(
                     src = words[:, 128 * u : 128 * u + 128] if widened_by[i, g] == "v" else words[:, u:256:2]
                     nc.tensor.transpose(tr[:, c : c + 128], src, ident[:])
 
-        def copy_x(i, eng):
-            dst = xg[i][:].bitcast(F32).rearrange("p (g c u) -> p g c u", g=2, u=2)
-            empty(("tr", i), eng, dst, lambda acc: acc[:].rearrange("p (g u c) -> p g c u", g=2, u=2))
+        def copy_x(i, eng, g0=0, g1=2):
+            dst = xg[i][:].bitcast(F32).rearrange("p (g c u) -> p g c u", g=2, u=2)[:, g0:g1]
+            empty(("tr", i), eng, dst, lambda acc: acc[:].rearrange("p (g u c) -> p g c u", g=2, u=2)[:, g0:g1], g1 == 2)
 
         def quant_x(i, g0=0, g1=2):
             words = slice(128 * g0, 128 * g1)
@@ -175,7 +175,7 @@ def tile_svftrandompatternsingularcoupling_d1p_kernel(
 
         def mask_test(h):
             dst = msk[h][:].rearrange("p (u c e) -> p u c e", u=2, e=2)
-            nc.vector.tensor_scalar(out=dst, in0=by_word(pat[:, 1024 * h : 1024 * h + 1024]), scalar1=0.25, scalar2=None, op0=ALU.is_lt)
+            nc.vector.tensor_scalar(out=dst, in0=by_word(pat[h][:]), scalar1=0.25, scalar2=None, op0=ALU.is_lt)
 
         def mask_apply(h):
             dst = msk[h][:].rearrange("p (u c e) -> p u c e", u=2, e=2)
@@ -187,14 +187,14 @@ def tile_svftrandompatternsingularcoupling_d1p_kernel(
             for s in range(4):
                 nc.tensor.transpose(tr[:, 128 * s : 128 * s + 128], words[:, 128 * s : 128 * s + 128], pident[:])
 
-        def copy_m(h, eng, c0=0, c1=P):
-            dst = msb[:].bitcast(F32).rearrange("p (c a u) -> p c a u", a=4, u=2)[:, c0:c1, 2 * h : 2 * h + 2, :]
-            view = lambda acc: acc[:].rearrange("p (u a c) -> p c a u", a=2, u=2)[:, c0:c1]
-            empty(("trm", h), eng, dst, view, c1 == P)
+        def copy_m(t, eng):
+            dst = msb[t][:].bitcast(F32).rearrange("p (c a u) -> p c a u", a=2, u=2)
+            view = lambda acc: acc[:].rearrange("p (u a c) -> p c a u", a=2, u=2)[:, 64 * (t % 2) : 64 * (t % 2) + 64]
+            empty(("trm", t // 2), eng, dst, view, t % 2 == 1)
 
         def quant_m(t):
             cols = slice(128 * t, 128 * t + 128)
-            nc.vector.quantize_mx(out=msq[:, cols].bitcast(X4), scales=mss[:, cols], in_=msb[:, 512 * t : 512 * t + 512])
+            nc.vector.quantize_mx(out=msq[:, cols].bitcast(X4), scales=mss[:, cols], in_=msb[t][:])
 
         def mm_n(slices, blocks):
             for t in slices:
@@ -253,8 +253,8 @@ def tile_svftrandompatternsingularcoupling_d1p_kernel(
         warm(vs[:, 0, :].bitcast(F32), 2)
         make_identity(nc, ident[:])
         nc.scalar.copy(
-            out=pident[:].rearrange("p (t q b) -> p t q b", t=4, q=16),
-            in_=ident[:].rearrange("p (q t b) -> p t q b", q=16, t=4),
+            out=pident[:].rearrange("p (t q b) -> p t q b", t=2, q=16),
+            in_=ident[:].rearrange("p (q t b) -> p t q b", q=16, t=2),
         )
         nc.sync.dma_start(out=xs[:], in_=x_scale.rearrange("(p i) j -> p (i j)", i=8))
         load_x(0, 1)
@@ -264,9 +264,10 @@ def tile_svftrandompatternsingularcoupling_d1p_kernel(
         load_scales(us, 4, u_scales)
         nc.sync.dma_start(out=uw[1][:].bitcast(I32), in_=u_src[:, 1, :])
         load_x(4, 1)
-        nc.sync.dma_start(out=pat[:], in_=p_rows)
         for h in (0, 1):
-            nc.sync.dma_start(out=mt[h][:], in_=m_rows[:, h, :])
+            nc.sync.dma_start(out=pat[h][:], in_=p_rows[h])
+        for h in (0, 1):
+            nc.sync.dma_start(out=mt[h][:], in_=m_rows[h])
         load_w(0)
         nc.sync.dma_start(out=vw[:].bitcast(I32), in_=v_src)
         load_scales(vs, 8, vt_scales)
@@ -283,64 +284,73 @@ def tile_svftrandompatternsingularcoupling_d1p_kernel(
         for i in range(4):
             turn_x(i)
             warm(ident[:].bitcast(BF16), 2 - i // 2)
-            copy_x(i, "s")
+            for g in (0, 1):
+                copy_x(i, "s", g, g + 1)
         permute_u(0)
         permute_u_scales()
         quant_x(0, 0, 1)
+        permute_u(1)
         quant_x(0, 1, 2)
-        permute_u(1, 0, 2)
-        permute_u(1, 2, 4)
-        quant_x(1, 0, 1)
-        quant_x(1, 1, 2)
+        for g in (0, 1):
+            quant_x(1, g, g + 1)
         widen(4, 0, "s")
-        quant_x(2)
         mask_test(0)
-        quant_x(3)
+        for g in (0, 1):
+            quant_x(2, g, g + 1)
+        mask_test(1)
+        for g in (0, 1):
+            quant_x(3, g, g + 1)
         for i in range(4):
             h_tile(i)
             copy_h(i, "s")
-        mask_test(1)
+        mask_apply(0)
+        turn_m(0)
         turn_x(4, (0,))
-        for h in (0, 1):
-            mask_apply(h)
-            turn_m(h)
+        mask_apply(1)
+        turn_m(1)
         widen(4, 1, "v")
         turn_x(4, (1,))
         quant_h(0)
-        copy_m(0, "s")
-        quant_h(1)
-        copy_m(1, "v", 0, 64)
-        copy_m(1, "v", 64, P)
+        copy_m(0, "v")
+        copy_m(1, "v")
+        copy_m(2, "s")
+        copy_m(3, "s")
         copy_x(4, "s")
-        for i in range(3):
+        for i in range(2):
             mm_b(i, (0,))
+        mm_b(2, (0,), halves=(0,))
+        quant_h(1)
         for t in range(4):
             quant_m(t)
+        for g in (0, 1):
+            quant_x(4, g, g + 1)
         quant_h(2)
-        quant_x(4)
         quant_h(3)
-        widen(5, 0, "v")
+        for c in range(3):
+            mm_n((0, 1), (c,))
         for c in range(8):
-            mm_n(range(4), (c,))
+            mm_n((2, 3) if c < 3 else range(4), (c,))
             copy_n(c, "v" if c in (1, 3, 5) else "s")
             if c == 3:
+                h_tile(4)
+                mm_b(2, (0,), halves=(1,))
+                copy_h(4, "s")
                 for k in range(4):
                     quant_n(k)
-        h_tile(4)
         mm_b(3, (0,))
-        copy_h(4, "s")
+        quant_h(4)
+        widen(5, 0, "v")
         for k in range(4, 8):
             quant_n(k)
         for i in range(4):
             mm_d(i, (0,))
             finish(i, 0, "s")
         widen(5, 1, "v")
-        quant_h(4)
         for i in (6, 7):
             widen(i, 0, "v")
             widen(i, 1, "v")
-        group(0, 512, "s")
         group(4, 0, "s")
+        group(0, 512, "s")
         for i in (5, 6, 7):
             turn_x(i)
             copy_x(i, "s" if i == 6 else "v")

@@ -47,7 +47,7 @@ def tile_svftrandompatternsingularcoupling_d1p_kernel(
         ws = [tile("ws%d" % h, [2, 512], U8) for h in (0, 1)]
         ident = tile("ident", [P], F32)
         pident = tile("pident", [P], F32)
-        msb = [tile("msb%d" % t, [R], BF16) for t in range(4)]
+        msb = tile("msb", [4 * R], BF16)
         msq = tile("msq", [R], U32)
         mss = tile("mss", [R], U8)
         nb = [tile("nb%d" % c, [512], BF16) for c in range(8)]
@@ -65,8 +65,8 @@ def tile_svftrandompatternsingularcoupling_d1p_kernel(
         ctx.enter_context(tc.manual_schedule())
 
         x_rows = x_bytes.rearrange("(p i) k -> p i k", i=8)
-        m_rows = m.rearrange("(q h j a) k -> h q j (a k)", h=2, j=8, a=2)
-        p_rows = pattern.rearrange("(q h j a) k -> h q j (a k)", h=2, j=8, a=2)
+        m_rows = m.rearrange("(p h a) k -> p h (a k)", h=2, a=2)
+        p_rows = pattern.rearrange("(p h a) k -> p h (a k)", h=2, a=2)
         out_rows = out.rearrange("(p i) n -> p i n", i=8)
         u_src = u_words.rearrange("g p n t -> p g (n t)").bitcast(I32)
         w_src = w0_words.rearrange("g p n t -> p g (n t)").bitcast(I32)
@@ -187,14 +187,14 @@ def tile_svftrandompatternsingularcoupling_d1p_kernel(
             for s in range(4):
                 nc.tensor.transpose(tr[:, 128 * s : 128 * s + 128], words[:, 128 * s : 128 * s + 128], pident[:])
 
-        def copy_m(t, eng):
-            dst = msb[t][:].bitcast(F32).rearrange("p (c a u) -> p c a u", a=2, u=2)
-            view = lambda acc: acc[:].rearrange("p (u a c) -> p c a u", a=2, u=2)[:, 64 * (t % 2) : 64 * (t % 2) + 64]
-            empty(("trm", t // 2), eng, dst, view, t % 2 == 1)
+        def copy_m(h, eng, c0=0, c1=P):
+            dst = msb[:].bitcast(F32).rearrange("p (c a u) -> p c a u", a=4, u=2)[:, c0:c1, 2 * h : 2 * h + 2, :]
+            view = lambda acc: acc[:].rearrange("p (u a c) -> p c a u", a=2, u=2)[:, c0:c1]
+            empty(("trm", h), eng, dst, view, c1 == P)
 
         def quant_m(t):
             cols = slice(128 * t, 128 * t + 128)
-            nc.vector.quantize_mx(out=msq[:, cols].bitcast(X4), scales=mss[:, cols], in_=msb[t][:])
+            nc.vector.quantize_mx(out=msq[:, cols].bitcast(X4), scales=mss[:, cols], in_=msb[:, 512 * t : 512 * t + 512])
 
         def mm_n(slices, blocks):
             for t in slices:
@@ -253,8 +253,8 @@ def tile_svftrandompatternsingularcoupling_d1p_kernel(
         warm(vs[:, 0, :].bitcast(F32), 2)
         make_identity(nc, ident[:])
         nc.scalar.copy(
-            out=pident[:].rearrange("p (t q b) -> p t q b", t=2, q=16),
-            in_=ident[:].rearrange("p (q t b) -> p t q b", q=16, t=2),
+            out=pident[:].rearrange("p (t q b) -> p t q b", t=4, q=16),
+            in_=ident[:].rearrange("p (q t b) -> p t q b", q=16, t=4),
         )
         nc.sync.dma_start(out=xs[:], in_=x_scale.rearrange("(p i) j -> p (i j)", i=8))
         load_x(0, 1)
@@ -265,9 +265,9 @@ def tile_svftrandompatternsingularcoupling_d1p_kernel(
         nc.sync.dma_start(out=uw[1][:].bitcast(I32), in_=u_src[:, 1, :])
         load_x(4, 1)
         for h in (0, 1):
-            nc.sync.dma_start(out=pat[h][:], in_=p_rows[h])
+            nc.sync.dma_start(out=pat[h][:], in_=p_rows[:, h, :])
         for h in (0, 1):
-            nc.sync.dma_start(out=mt[h][:], in_=m_rows[h])
+            nc.sync.dma_start(out=mt[h][:], in_=m_rows[:, h, :])
         load_w(0)
         nc.sync.dma_start(out=vw[:].bitcast(I32), in_=v_src)
         load_scales(vs, 8, vt_scales)
@@ -303,18 +303,17 @@ def tile_svftrandompatternsingularcoupling_d1p_kernel(
         for i in range(4):
             h_tile(i)
             copy_h(i, "s")
-        mask_apply(0)
-        turn_m(0)
         turn_x(4, (0,))
-        mask_apply(1)
-        turn_m(1)
+        for h in (0, 1):
+            mask_apply(h)
+            turn_m(h)
         widen(4, 1, "v")
         turn_x(4, (1,))
         quant_h(0)
-        copy_m(0, "v")
-        copy_m(1, "v")
-        copy_m(2, "s")
-        copy_m(3, "s")
+        copy_m(0, "v", 0, 64)
+        copy_m(0, "v", 64, P)
+        for t in range(4):
+            copy_m(1, "s", 32 * t, 32 * t + 32)
         copy_x(4, "s")
         for i in range(2):
             mm_b(i, (0,))
@@ -326,10 +325,11 @@ def tile_svftrandompatternsingularcoupling_d1p_kernel(
             quant_x(4, g, g + 1)
         quant_h(2)
         quant_h(3)
-        for c in range(3):
-            mm_n((0, 1), (c,))
         for c in range(8):
-            mm_n((2, 3) if c < 3 else range(4), (c,))
+            if c == 0:
+                mm_n(range(4), range(2))
+            elif c >= 2:
+                mm_n(range(4), (c,))
             copy_n(c, "v" if c in (1, 3, 5) else "s")
             if c == 3:
                 h_tile(4)

@@ -325,6 +325,7 @@ def tile_svftrandompatternsingularcoupling_d1p_kernel(
             quant_x(4, g, g + 1)
         quant_h(2)
         quant_h(3)
+        widen(5, 0, "v")
         for c in range(8):
             if c == 0:
                 mm_n(range(4), range(2))
@@ -337,25 +338,29 @@ def tile_svftrandompatternsingularcoupling_d1p_kernel(
                 copy_h(4, "s")
                 for k in range(4):
                     quant_n(k)
+                widen(5, 1, "v")
         mm_b(3, (0,))
         quant_h(4)
-        widen(5, 0, "v")
+        widen(6, 0, "v")
         for k in range(4, 8):
             quant_n(k)
         for i in range(4):
             mm_d(i, (0,))
             finish(i, 0, "s")
-        widen(5, 1, "v")
-        for i in (6, 7):
-            widen(i, 0, "v")
-            widen(i, 1, "v")
+        widen(6, 1, "v")
+        for g in (0, 1):
+            widen(7, g, "v")
         group(4, 0, "s")
         group(0, 512, "s")
         for i in (5, 6, 7):
             turn_x(i)
-            copy_x(i, "s" if i == 6 else "v")
-            if i > 5:
-                quant_x(i - 1)
+        for g in (0, 1):
+            copy_x(5, "v", g, g + 1)
+        copy_x(6, "s")
+        for g in (0, 1):
+            quant_x(5, g, g + 1)
+        copy_x(7, "v")
+        quant_x(6)
         quant_x(7)
         for i in range(1, 5):
             group(i, 512, "s")

@@ -34,7 +34,7 @@ def tile_svftrandompatternsingularcoupling_d1p_kernel(
 
         xb = tile("xb", [8, D], U8)
         xs = tile("xs", [64], F32)
-        pat = [tile("pat%d" % h, [2 * R], BF16) for h in (0, 1)]
+        pat = tile("pat", [4 * R], BF16)
         mt = [tile("mt%d" % h, [2 * R], BF16) for h in (0, 1)]
         msk = [tile("msk%d" % h, [2 * R], BF16) for h in (0, 1)]
         uw = [tile("uw%d" % g, [R], U32) for g in (0, 1)]
@@ -66,7 +66,7 @@ def tile_svftrandompatternsingularcoupling_d1p_kernel(
 
         x_rows = x_bytes.rearrange("(p i) k -> p i k", i=8)
         m_rows = m.rearrange("(p h a) k -> p h (a k)", h=2, a=2)
-        p_rows = pattern.rearrange("(p h a) k -> p h (a k)", h=2, a=2)
+        p_rows = pattern.rearrange("(p a) k -> p (a k)", a=4)
         out_rows = out.rearrange("(p i) n -> p i n", i=8)
         u_src = u_words.rearrange("g p n t -> p g (n t)").bitcast(I32)
         w_src = w0_words.rearrange("g p n t -> p g (n t)").bitcast(I32)
@@ -80,9 +80,10 @@ def tile_svftrandompatternsingularcoupling_d1p_kernel(
             for r in range(4):
                 nc.sync.dma_start(out=plane[first + r : P : 32, :, :].bitcast(I32), in_=rows[r].bitcast(I32))
 
-        def load_w(h):
+        def load_w(h, parts):
             load_scales(ws[h], 12, w0_scales[:, :, 512 * h : 512 * h + 512])
-            nc.sync.dma_start(out=ww[h][:].bitcast(I32), in_=w_src[:, :, 512 * h : 512 * h + 512])
+            for gs in parts:
+                nc.sync.dma_start(out=ww[h][:, gs, :].bitcast(I32), in_=w_src[:, gs, 512 * h : 512 * h + 512])
 
         live = {}
         idle = list(range(8))
@@ -175,7 +176,7 @@ def tile_svftrandompatternsingularcoupling_d1p_kernel(
 
         def mask_test(h):
             dst = msk[h][:].rearrange("p (u c e) -> p u c e", u=2, e=2)
-            nc.vector.tensor_scalar(out=dst, in0=by_word(pat[h][:]), scalar1=0.25, scalar2=None, op0=ALU.is_lt)
+            nc.vector.tensor_scalar(out=dst, in0=by_word(pat[:, 1024 * h : 1024 * h + 1024]), scalar1=0.25, scalar2=None, op0=ALU.is_lt)
 
         def mask_apply(h):
             dst = msk[h][:].rearrange("p (u c e) -> p u c e", u=2, e=2)
@@ -263,16 +264,16 @@ def tile_svftrandompatternsingularcoupling_d1p_kernel(
         nc.sync.dma_start(out=uw[0][:].bitcast(I32), in_=u_src[:, 0, :])
         load_scales(us, 4, u_scales)
         nc.sync.dma_start(out=uw[1][:].bitcast(I32), in_=u_src[:, 1, :])
+        nc.sync.dma_start(out=pat[:], in_=p_rows)
         load_x(4, 1)
         for h in (0, 1):
-            nc.sync.dma_start(out=pat[h][:], in_=p_rows[:, h, :])
-        for h in (0, 1):
             nc.sync.dma_start(out=mt[h][:], in_=m_rows[:, h, :])
-        load_w(0)
-        nc.sync.dma_start(out=vw[:].bitcast(I32), in_=v_src)
+        load_w(0, (slice(0, 1), slice(1, 2)))
+        nc.sync.dma_start(out=vw[:, 0:512].bitcast(I32), in_=v_src[:, 0:512])
         load_scales(vs, 8, vt_scales)
+        nc.sync.dma_start(out=vw[:, 512:N].bitcast(I32), in_=v_src[:, 512:N])
         load_x(5, 3)
-        load_w(1)
+        load_w(1, (slice(0, 2),))
 
         def h_tile(i):
             for g in (0, 1):
@@ -294,12 +295,10 @@ def tile_svftrandompatternsingularcoupling_d1p_kernel(
         for g in (0, 1):
             quant_x(1, g, g + 1)
         widen(4, 0, "s")
-        mask_test(0)
-        for g in (0, 1):
-            quant_x(2, g, g + 1)
-        mask_test(1)
-        for g in (0, 1):
-            quant_x(3, g, g + 1)
+        for i in (2, 3):
+            quant_x(i, 0, 1)
+            mask_test(i - 2)
+            quant_x(i, 1, 2)
         for i in range(4):
             h_tile(i)
             copy_h(i, "s")
@@ -315,9 +314,9 @@ def tile_svftrandompatternsingularcoupling_d1p_kernel(
         for t in range(4):
             copy_m(1, "s", 32 * t, 32 * t + 32)
         copy_x(4, "s")
-        for i in range(2):
-            mm_b(i, (0,))
-        mm_b(2, (0,), halves=(0,))
+        for g in (0, 1):
+            for i in range(3 - g):
+                mm_b(i, (0,), halves=(g,))
         quant_h(1)
         for t in range(4):
             quant_m(t)
@@ -325,7 +324,6 @@ def tile_svftrandompatternsingularcoupling_d1p_kernel(
             quant_x(4, g, g + 1)
         quant_h(2)
         quant_h(3)
-        widen(5, 0, "v")
         for c in range(8):
             if c == 0:
                 mm_n(range(4), range(2))
@@ -338,18 +336,18 @@ def tile_svftrandompatternsingularcoupling_d1p_kernel(
                 copy_h(4, "s")
                 for k in range(4):
                     quant_n(k)
-                widen(5, 1, "v")
+                widen(5, 0, "v")
         mm_b(3, (0,))
         quant_h(4)
-        widen(6, 0, "v")
+        widen(5, 1, "v")
         for k in range(4, 8):
             quant_n(k)
         for i in range(4):
             mm_d(i, (0,))
             finish(i, 0, "s")
-        widen(6, 1, "v")
-        for g in (0, 1):
-            widen(7, g, "v")
+        for i in (6, 7):
+            for g in (0, 1):
+                widen(i, g, "v")
         group(4, 0, "s")
         group(0, 512, "s")
         for i in (5, 6, 7):

@@ -7,6 +7,12 @@ T, D, R, N = 1024, 1024, 512, 1024
 FLOPS = 2 * (R * R * N + T * D * R + T * R * N + T * D * N)
 
 P = 128
+TILES = T // P
+BANKS = 8
+HALF = 512
+KEEP_BELOW = 0.25
+U_ROWS, V_ROWS, W_ROWS, N_ROWS = 4, 8, 12, 4
+
 F32 = mybir.dt.float32
 BF16 = mybir.dt.bfloat16
 I32 = mybir.dt.int32
@@ -29,48 +35,49 @@ def tile_svftrandompatternsingularcoupling_d1p_kernel(
         def tile(name, shape, dtype):
             return keep.tile([P] + shape, dtype, align_bytes=256, name=name)
 
-        def shifted(name, words):
-            return tile(name, [16 + words], U32)[:, 16:]
-
-        xb = tile("xb", [8, D], U8)
-        xs = tile("xs", [64], F32)
+        xb = tile("xb", [TILES, D], U8)
+        xs = tile("xs", [TILES * 8], F32)
         pat = tile("pat", [4 * R], BF16)
         mt = [tile("mt%d" % h, [2 * R], BF16) for h in (0, 1)]
         msk = [tile("msk%d" % h, [2 * R], BF16) for h in (0, 1)]
         uw = [tile("uw%d" % g, [R], U32) for g in (0, 1)]
-        up = [shifted("up%d" % g, R) for g in (0, 1)]
+        up = [tile("up%d" % g, [R], U32) for g in (0, 1)]
         us = tile("us", [2, R], U8)
         usp = tile("usp", [2, R], U8)
-        vw = shifted("vw", N)
+        vw = tile("vw", [N], U32)
         vs = tile("vs", [1, N], U8)
-        ww = [shifted("ww%d" % h, 1024).rearrange("p (g n) -> p g n", g=2) for h in (0, 1)]
-        ws = [tile("ws%d" % h, [2, 512], U8) for h in (0, 1)]
+        ww = [tile("ww%d" % h, [2, HALF], U32) for h in (0, 1)]
+        ws = [tile("ws%d" % h, [2, HALF], U8) for h in (0, 1)]
         ident = tile("ident", [P], F32)
         pident = tile("pident", [P], F32)
         msb = tile("msb", [4 * R], BF16)
         msq = tile("msq", [R], U32)
         mss = tile("mss", [R], U8)
-        nb = [tile("nb%d" % c, [512], BF16) for c in range(8)]
-        nq = shifted("nq", N)
+        nb = [tile("nb%d" % c, [4 * P], BF16) for c in range(N // P)]
+        nq = tile("nq", [N], U32)
         nsc = tile("nsc", [N], U8)
-        xw = [[tile("xw%d%d" % (i, g), [512], BF16) for g in (0, 1)] for i in range(8)]
-        xg = [tile("xg%d" % i, [D], BF16) for i in range(8)]
-        xq = [tile("xq%d" % i, [256], U32) for i in range(8)]
-        xsc = [tile("xsc%d" % i, [256], U8) for i in range(8)]
-        hb = [tile("hb%d" % i, [512], BF16) for i in range(8)]
-        hq = [tile("hq%d" % i, [P], U32) for i in range(8)]
-        hs = [tile("hs%d" % i, [P], U8) for i in range(8)]
-        osb = [tile("osb%d" % i, [N], F32) for i in range(8)]
+        xw = [[tile("xw%d%d" % (i, g), [HALF], BF16) for g in (0, 1)] for i in range(TILES)]
+        xg = [tile("xg%d" % i, [D], BF16) for i in range(TILES)]
+        xq = [tile("xq%d" % i, [2 * P], U32) for i in range(TILES)]
+        xsc = [tile("xsc%d" % i, [2 * P], U8) for i in range(TILES)]
+        hb = [tile("hb%d" % i, [4 * P], BF16) for i in range(TILES)]
+        hq = [tile("hq%d" % i, [P], U32) for i in range(TILES)]
+        hs = [tile("hs%d" % i, [P], U8) for i in range(TILES)]
+        osb = [tile("osb%d" % i, [N], F32) for i in range(TILES)]
 
         ctx.enter_context(tc.manual_schedule())
 
-        x_rows = x_bytes.rearrange("(p i) k -> p i k", i=8)
+        x_rows = x_bytes.rearrange("(p i) k -> p i k", i=TILES)
         m_rows = m.rearrange("(p h a) k -> p h (a k)", h=2, a=2)
         p_rows = pattern.rearrange("(p a) k -> p (a k)", a=4)
-        out_rows = out.rearrange("(p i) n -> p i n", i=8)
+        out_rows = out.rearrange("(p i) n -> p i n", i=TILES)
         u_src = u_words.rearrange("g p n t -> p g (n t)").bitcast(I32)
         w_src = w0_words.rearrange("g p n t -> p g (n t)").bitcast(I32)
         v_src = vt_words[0].rearrange("p n t -> p (n t)").bitcast(I32)
+
+        def span(start, width):
+            return slice(start, start + width)
+
 
         def load_x(i, count):
             nc.sync.dma_start(out=xb[:, i : i + count, :], in_=x_rows[:, i : i + count, :])
@@ -81,17 +88,22 @@ def tile_svftrandompatternsingularcoupling_d1p_kernel(
                 nc.sync.dma_start(out=plane[first + r : P : 32, :, :].bitcast(I32), in_=rows[r].bitcast(I32))
 
         def load_w(h, parts):
-            load_scales(ws[h], 12, w0_scales[:, :, 512 * h : 512 * h + 512])
+            cols = span(HALF * h, HALF)
+            load_scales(ws[h], W_ROWS, w0_scales[:, :, cols])
             for gs in parts:
-                nc.sync.dma_start(out=ww[h][:, gs, :].bitcast(I32), in_=w_src[:, gs, 512 * h : 512 * h + 512])
+                nc.sync.dma_start(out=ww[h][:, gs, :].bitcast(I32), in_=w_src[:, gs, cols])
+
+        def load_v(h):
+            cols = span(HALF * h, HALF)
+            nc.sync.dma_start(out=vw[:, cols].bitcast(I32), in_=v_src[:, cols])
+
 
         live = {}
-        idle = list(range(8))
+        idle = list(range(BANKS))
 
         def take(key):
-            b = idle[0]
-            idle.remove(b)
-            live[key] = (b, psum.tile([P, 512], F32, tag="bank%d" % b, name="bank"))
+            b = idle.pop(0)
+            live[key] = (b, psum.tile([P, HALF], F32, tag="bank%d" % b, name="bank"))
             return live[key][1]
 
         def bank(key):
@@ -116,11 +128,15 @@ def tile_svftrandompatternsingularcoupling_d1p_kernel(
 
         def mx(acc, lhs, rhs, start, stop):
             nc.tensor.matmul_mx(
-                out=acc, lhsT=lhs[0].bitcast(X4), lhsT_scale=lhs[1], rhs=rhs[0].bitcast(X4), rhs_scale=rhs[1], start=start, stop=stop
+                out=acc,
+                lhsT=lhs[0].bitcast(X4),
+                lhsT_scale=lhs[1],
+                rhs=rhs[0].bitcast(X4),
+                rhs_scale=rhs[1],
+                start=start,
+                stop=stop,
             )
 
-        def x_operand(i, g):
-            return xq[i][:, 128 * g : 128 * g + 128], xsc[i][:, 128 * g : 128 * g + 128]
 
         widened_by = {}
 
@@ -129,40 +145,48 @@ def tile_svftrandompatternsingularcoupling_d1p_kernel(
             pairs = xw[i][g][:].rearrange("p (u c e) -> p c u e", u=2, e=2)
             for b in range(4):
                 j = 4 * g + b
-                src = xb[:, i, 128 * j : 128 * j + 128].bitcast(FP8)
-                sc = xs[:, 8 * i + j : 8 * i + j + 1]
+                src = xb[:, i, span(P * j, P)].bitcast(FP8)
+                sc = xs[:, span(8 * i + j, 1)]
                 if eng == "v":
                     nc.vector.tensor_scalar(
-                        out=pairs[:, 32 * b : 32 * b + 32, :, :],
+                        out=pairs[:, span(32 * b, 32), :, :],
                         in0=src.rearrange("p (c u e) -> p c u e", u=2, e=2),
                         scalar1=sc,
                         scalar2=None,
                         op0=ALU.mult,
                     )
                 else:
-                    nc.scalar.activation(out=xw[i][g][:, 128 * b : 128 * b + 128], in_=src, func=ACT.Copy, scale=sc)
+                    nc.scalar.activation(out=xw[i][g][:, span(P * b, P)], in_=src, func=ACT.Copy, scale=sc)
+
+        def x_bank(i, g):
+            return ("tr", i, g if i == 0 else 0)
 
         def turn_x(i, halves=(0, 1)):
-            tr = bank(("tr", i))
             for g in halves:
+                tr = bank(x_bank(i, g))
                 words = xw[i][g][:].bitcast(F32)
                 for u in (0, 1):
-                    c = 128 * (2 * g + u)
-                    src = words[:, 128 * u : 128 * u + 128] if widened_by[i, g] == "v" else words[:, u:256:2]
-                    nc.tensor.transpose(tr[:, c : c + 128], src, ident[:])
+                    src = words[:, span(P * u, P)] if widened_by[i, g] == "v" else words[:, u : 2 * P : 2]
+                    nc.tensor.transpose(tr[:, span(P * (2 * g + u), P)], src, ident[:])
 
         def copy_x(i, eng, g0=0, g1=2):
             dst = xg[i][:].bitcast(F32).rearrange("p (g c u) -> p g c u", g=2, u=2)[:, g0:g1]
-            empty(("tr", i), eng, dst, lambda acc: acc[:].rearrange("p (g u c) -> p g c u", g=2, u=2)[:, g0:g1], g1 == 2)
+            view = lambda acc: acc[:].rearrange("p (g u c) -> p g c u", g=2, u=2)[:, g0:g1]
+            empty(x_bank(i, g0), eng, dst, view, g1 == 2 or i == 0)
 
         def quant_x(i, g0=0, g1=2):
-            words = slice(128 * g0, 128 * g1)
-            nc.vector.quantize_mx(out=xq[i][:, words].bitcast(X4), scales=xsc[i][:, words], in_=xg[i][:, 512 * g0 : 512 * g1])
+            words = slice(P * g0, P * g1)
+            src = xg[i][:, HALF * g0 : HALF * g1]
+            nc.vector.quantize_mx(out=xq[i][:, words].bitcast(X4), scales=xsc[i][:, words], in_=src)
 
-        def permute_u(g, t0=0, t1=4):
+        def x_operand(i, g):
+            return xq[i][:, span(P * g, P)], xsc[i][:, span(P * g, P)]
+
+
+        def permute_u(g):
             nc.vector.tensor_copy(
-                out=up[g][:].bitcast(I32).rearrange("p (t q j) -> p t q j", t=4, q=16)[:, t0:t1],
-                in_=uw[g][:].bitcast(I32).rearrange("p (q t j) -> p t q j", q=16, t=4)[:, t0:t1],
+                out=up[g][:].bitcast(I32).rearrange("p (t q j) -> p t q j", t=4, q=16),
+                in_=uw[g][:].bitcast(I32).rearrange("p (q t j) -> p t q j", q=16, t=4),
             )
 
         def permute_u_scales():
@@ -171,83 +195,83 @@ def tile_svftrandompatternsingularcoupling_d1p_kernel(
                 in_=us[:].bitcast(I32).rearrange("p g (q t j) -> p g t q j", q=16, t=4),
             )
 
+
         def by_word(t):
             return t.rearrange("p (c u e) -> p u c e", u=2, e=2)
 
         def mask_test(h):
             dst = msk[h][:].rearrange("p (u c e) -> p u c e", u=2, e=2)
-            nc.vector.tensor_scalar(out=dst, in0=by_word(pat[:, 1024 * h : 1024 * h + 1024]), scalar1=0.25, scalar2=None, op0=ALU.is_lt)
+            src = by_word(pat[:, span(2 * R * h, 2 * R)])
+            nc.vector.tensor_scalar(out=dst, in0=src, scalar1=KEEP_BELOW, scalar2=None, op0=ALU.is_lt)
 
-        def mask_apply(h):
-            dst = msk[h][:].rearrange("p (u c e) -> p u c e", u=2, e=2)
-            nc.vector.tensor_tensor(out=dst, in0=dst, in1=by_word(mt[h][:]), op=ALU.mult)
+        def mask_apply(h, u0=0, u1=2):
+            dst = msk[h][:].rearrange("p (u c e) -> p u c e", u=2, e=2)[:, u0:u1]
+            nc.vector.tensor_tensor(out=dst, in0=dst, in1=by_word(mt[h][:])[:, u0:u1], op=ALU.mult)
 
         def turn_m(h):
             tr = take(("trm", h))
             words = msk[h][:].bitcast(F32)
             for s in range(4):
-                nc.tensor.transpose(tr[:, 128 * s : 128 * s + 128], words[:, 128 * s : 128 * s + 128], pident[:])
+                nc.tensor.transpose(tr[:, span(P * s, P)], words[:, span(P * s, P)], pident[:])
 
-        def copy_m(h, eng, c0=0, c1=P):
-            dst = msb[:].bitcast(F32).rearrange("p (c a u) -> p c a u", a=4, u=2)[:, c0:c1, 2 * h : 2 * h + 2, :]
-            view = lambda acc: acc[:].rearrange("p (u a c) -> p c a u", a=2, u=2)[:, c0:c1]
-            empty(("trm", h), eng, dst, view, c1 == P)
+        def copy_m(h, eng, parts):
+            dst = msb[:].bitcast(F32).rearrange("p (c a u) -> p c a u", a=4, u=2)
+            for part in range(parts):
+                cols = span(P // parts * part, P // parts)
+                view = lambda acc: acc[:].rearrange("p (u a c) -> p c a u", a=2, u=2)[:, cols]
+                empty(("trm", h), eng, dst[:, cols, span(2 * h, 2), :], view, part == parts - 1)
 
         def quant_m(t):
-            cols = slice(128 * t, 128 * t + 128)
-            nc.vector.quantize_mx(out=msq[:, cols].bitcast(X4), scales=mss[:, cols], in_=msb[:, 512 * t : 512 * t + 512])
+            cols = span(P * t, P)
+            nc.vector.quantize_mx(out=msq[:, cols].bitcast(X4), scales=mss[:, cols], in_=msb[:, span(R * t, R)])
 
-        def mm_n(slices, blocks):
-            for t in slices:
-                rows = slice(128 * t, 128 * t + 128)
+
+        def interleave(key, eng, dst):
+            view = lambda acc: acc[:].rearrange("p (t n) -> p n t", t=4)
+            empty(key, eng, dst[:].rearrange("p (n t) -> p n t", t=4), view)
+
+        def mm_n(blocks):
+            for t in range(4):
+                rows = span(P * t, P)
                 for c in blocks:
-                    cols = slice(128 * c, 128 * c + 128)
-                    mx(bank(("n", c))[:, rows], (msq[:, rows], mss[:, rows]), (vw[:, cols], vs[8:P, 0, cols]), True, True)
-
-        def copy_n(c, eng):
-            dst = nb[c][:].rearrange("p (n t) -> p n t", t=4)
-            empty(("n", c), eng, dst, lambda acc: acc[:].rearrange("p (t n) -> p n t", t=4))
+                    cols = span(P * c, P)
+                    rhs = (vw[:, cols], vs[V_ROWS:P, 0, cols])
+                    mx(bank(("n", c))[:, rows], (msq[:, rows], mss[:, rows]), rhs, True, True)
 
         def quant_n(c):
-            cols = slice(128 * c, 128 * c + 128)
-            nc.vector.quantize_mx(out=nq[:, cols].bitcast(X4), scales=nsc[4:P, cols], in_=nb[c][:])
+            cols = span(P * c, P)
+            nc.vector.quantize_mx(out=nq[:, cols].bitcast(X4), scales=nsc[N_ROWS:P, cols], in_=nb[c][:])
 
-        def mm_h(g, tiles):
-            opened = [("h", i) in live for i in tiles]
-            for t in range(4):
-                rows = slice(128 * t, 128 * t + 128)
-                for i, second in zip(tiles, opened):
-                    first_pass, last_pass = not second and t == 0, second and t == 3
-                    mx(bank(("h", i))[:, rows], (up[g][:, rows], usp[4:P, g, rows]), x_operand(i, g), first_pass, last_pass)
-
-        def copy_h(i, eng):
-            dst = hb[i][:].rearrange("p (n t) -> p n t", t=4)
-            empty(("h", i), eng, dst, lambda acc: acc[:].rearrange("p (t n) -> p n t", t=4))
+        def mm_h(i):
+            acc = take(("h", i))
+            for g in (0, 1):
+                for t in range(4):
+                    rows = span(P * t, P)
+                    lhs = (up[g][:, rows], usp[U_ROWS:P, g, rows])
+                    mx(acc[:, rows], lhs, x_operand(i, g), (g, t) == (0, 0), (g, t) == (1, 3))
 
         def quant_h(i):
             nc.vector.quantize_mx(out=hq[i][:].bitcast(X4), scales=hs[i][:], in_=hb[i][:])
 
-        def mm_b(i, starts, width=512, halves=(0, 1)):
+
+        def mm_b(i, c0, width=HALF, halves=(0, 1)):
+            h, cols = c0 // HALF, span(c0 % HALF, width)
             for g in halves:
-                for c0 in starts:
-                    half, cols = c0 // 512, slice(c0 % 512, c0 % 512 + width)
-                    mx(bank(("o", i, c0))[:, 0:width], x_operand(i, g), (ww[half][:, g, cols], ws[half][12:P, g, cols]), g == 0, False)
+                rhs = (ww[h][:, g, cols], ws[h][W_ROWS:P, g, cols])
+                mx(bank(("o", i, c0))[:, 0:width], x_operand(i, g), rhs, g == 0, False)
 
-        def mm_d(i, starts, width=512):
-            for c0 in starts:
-                cols = slice(c0, c0 + width)
-                mx(bank(("o", i, c0))[:, 0:width], (hq[i][:], hs[i][:]), (nq[:, cols], nsc[4:P, cols]), False, True)
-
-        def finish(i, c0, eng, width=512):
-            empty(("o", i, c0), eng, osb[i][:, c0 : c0 + width], lambda acc: acc[:, 0:width])
-            if (c0 + width) % 512 == 0:
-                cols = slice(c0 + width - 512, c0 + width)
+        def close(i, c0, eng, width=HALF):
+            cols = span(c0, width)
+            mx(bank(("o", i, c0))[:, 0:width], (hq[i][:], hs[i][:]), (nq[:, cols], nsc[N_ROWS:P, cols]), False, True)
+            empty(("o", i, c0), eng, osb[i][:, cols], lambda acc: acc[:, 0:width])
+            if (c0 + width) % HALF == 0:
+                cols = span(c0 + width - HALF, HALF)
                 nc.sync.dma_start(out=out_rows[:, i, cols], in_=osb[i][:, cols])
 
-        def group(i, c0, eng):
-            mm_b(i, (c0,))
-            mm_d(i, (c0,))
-            finish(i, c0, eng)
+        def group(i, c0, eng, width=HALF):
+            mm_b(i, c0, width)
+            close(i, c0, eng, width)
+
 
         for plane in (us, vs, ws[0], ws[1]):
             nc.vector.memset(plane[:].bitcast(I32), 0)
@@ -257,34 +281,35 @@ def tile_svftrandompatternsingularcoupling_d1p_kernel(
             out=pident[:].rearrange("p (t q b) -> p t q b", t=4, q=16),
             in_=ident[:].rearrange("p (q t b) -> p t q b", q=16, t=4),
         )
-        nc.sync.dma_start(out=xs[:], in_=x_scale.rearrange("(p i) j -> p (i j)", i=8))
+
+        nc.sync.dma_start(out=xs[:], in_=x_scale.rearrange("(p i) j -> p (i j)", i=TILES))
         load_x(0, 1)
         load_x(1, 1)
         load_x(2, 2)
         nc.sync.dma_start(out=uw[0][:].bitcast(I32), in_=u_src[:, 0, :])
-        load_scales(us, 4, u_scales)
+        load_scales(us, U_ROWS, u_scales)
         nc.sync.dma_start(out=uw[1][:].bitcast(I32), in_=u_src[:, 1, :])
         nc.sync.dma_start(out=pat[:], in_=p_rows)
         load_x(4, 1)
         for h in (0, 1):
             nc.sync.dma_start(out=mt[h][:], in_=m_rows[:, h, :])
         load_w(0, (slice(0, 1), slice(1, 2)))
-        nc.sync.dma_start(out=vw[:, 0:512].bitcast(I32), in_=v_src[:, 0:512])
-        load_scales(vs, 8, vt_scales)
-        nc.sync.dma_start(out=vw[:, 512:N].bitcast(I32), in_=v_src[:, 512:N])
+        load_v(0)
+        load_scales(vs, V_ROWS, vt_scales)
+        load_v(1)
         load_x(5, 3)
         load_w(1, (slice(0, 2),))
-
-        def h_tile(i):
-            for g in (0, 1):
-                mm_h(g, (i,))
 
         for i in range(4):
             widen(i, 0, "v")
             widen(i, 1, "s" if i in (1, 2) else "v")
         for i in range(4):
-            turn_x(i)
-            warm(ident[:].bitcast(BF16), 2 - i // 2)
+            turn_x(i, (0,))
+            if i == 0:
+                warm(ident[:].bitcast(BF16), 2)
+            turn_x(i, (1,))
+            if i > 0:
+                warm(ident[:].bitcast(BF16), 2 - i // 2)
             for g in (0, 1):
                 copy_x(i, "s", g, g + 1)
         permute_u(0)
@@ -300,23 +325,24 @@ def tile_svftrandompatternsingularcoupling_d1p_kernel(
             mask_test(i - 2)
             quant_x(i, 1, 2)
         for i in range(4):
-            h_tile(i)
-            copy_h(i, "s")
+            mm_h(i)
+            interleave(("h", i), "s", hb[i])
+
         turn_x(4, (0,))
-        for h in (0, 1):
-            mask_apply(h)
-            turn_m(h)
+        mask_apply(0)
+        turn_m(0)
+        for u in (0, 1):
+            mask_apply(1, u, u + 1)
+        turn_m(1)
         widen(4, 1, "v")
         turn_x(4, (1,))
         quant_h(0)
-        copy_m(0, "v", 0, 64)
-        copy_m(0, "v", 64, P)
-        for t in range(4):
-            copy_m(1, "s", 32 * t, 32 * t + 32)
+        copy_m(0, "v", 2)
+        copy_m(1, "s", 4)
         copy_x(4, "s")
         for g in (0, 1):
             for i in range(3 - g):
-                mm_b(i, (0,), halves=(g,))
+                mm_b(i, 0, halves=(g,))
         quant_h(1)
         for t in range(4):
             quant_m(t)
@@ -324,32 +350,32 @@ def tile_svftrandompatternsingularcoupling_d1p_kernel(
             quant_x(4, g, g + 1)
         quant_h(2)
         quant_h(3)
-        for c in range(8):
-            if c == 0:
-                mm_n(range(4), range(2))
-            elif c >= 2:
-                mm_n(range(4), (c,))
-            copy_n(c, "v" if c in (1, 3, 5) else "s")
+
+        mm_n((0, 1))
+        for c in range(N // P):
+            if c > 1:
+                mm_n((c,))
+            interleave(("n", c), "v" if c in (1, 3, 5) else "s", nb[c])
             if c == 3:
-                h_tile(4)
-                mm_b(2, (0,), halves=(1,))
-                copy_h(4, "s")
+                mm_h(4)
+                mm_b(2, 0, halves=(1,))
+                interleave(("h", 4), "s", hb[4])
                 for k in range(4):
                     quant_n(k)
                 widen(5, 0, "v")
-        mm_b(3, (0,))
+        mm_b(3, 0)
         quant_h(4)
         widen(5, 1, "v")
         for k in range(4, 8):
             quant_n(k)
         for i in range(4):
-            mm_d(i, (0,))
-            finish(i, 0, "s")
+            close(i, 0, "s")
         for i in (6, 7):
             for g in (0, 1):
                 widen(i, g, "v")
         group(4, 0, "s")
-        group(0, 512, "s")
+        group(0, HALF, "s")
+
         for i in (5, 6, 7):
             turn_x(i)
         for g in (0, 1):
@@ -361,17 +387,16 @@ def tile_svftrandompatternsingularcoupling_d1p_kernel(
         quant_x(6)
         quant_x(7)
         for i in range(1, 5):
-            group(i, 512, "s")
+            group(i, HALF, "s")
             if i > 2:
                 quant_h(i + 2)
             if i > 1:
-                h_tile(i + 3)
-                copy_h(i + 3, "v")
+                mm_h(i + 3)
+                interleave(("h", i + 3), "v", hb[i + 3])
         group(5, 0, "s")
         quant_h(7)
-        group(5, 512, "v")
+        group(5, HALF, "v")
+
         for i in (6, 7):
             for k in range(4):
-                mm_b(i, (256 * k,), 256)
-                mm_d(i, (256 * k,), 256)
-                finish(i, 256 * k, "v" if k % 2 else "s", 256)
+                group(i, HALF // 2 * k, "v" if k % 2 else "s", HALF // 2)

@@ -264,13 +264,14 @@ def tile_svftrandompatternsingularcoupling_d1p_kernel(
             cols = span(c0, width)
             mx(bank(("o", i, c0))[:, 0:width], (hq[i][:], hs[i][:]), (nq[:, cols], nsc[N_ROWS:P, cols]), False, True)
             empty(("o", i, c0), eng, osb[i][:, cols], lambda acc: acc[:, 0:width])
-            if (c0 + width) % HALF == 0:
-                cols = span(c0 + width - HALF, HALF)
-                nc.sync.dma_start(out=out_rows[:, i, cols], in_=osb[i][:, cols])
 
         def group(i, c0, eng, width=HALF):
             mm_b(i, c0, width)
             close(i, c0, eng, width)
+
+        def store(i, c0, width=HALF):
+            cols = span(c0, width)
+            nc.sync.dma_start(out=out_rows[:, i, cols], in_=osb[i][:, cols])
 
 
         for plane in (us, vs, ws[0], ws[1]):
@@ -370,11 +371,15 @@ def tile_svftrandompatternsingularcoupling_d1p_kernel(
             quant_n(k)
         for i in range(4):
             close(i, 0, "s")
+            if i > 0:
+                store(i, 0)
         for i in (6, 7):
             for g in (0, 1):
                 widen(i, g, "v")
         group(4, 0, "s")
+        store(4, 0)
         group(0, HALF, "s")
+        store(0, 0, N)
 
         for i in (5, 6, 7):
             turn_x(i)
@@ -388,15 +393,23 @@ def tile_svftrandompatternsingularcoupling_d1p_kernel(
         quant_x(7)
         for i in range(1, 5):
             group(i, HALF, "s")
+            store(i, HALF)
             if i > 2:
                 quant_h(i + 2)
             if i > 1:
                 mm_h(i + 3)
                 interleave(("h", i + 3), "v", hb[i + 3])
         group(5, 0, "s")
+        store(5, 0)
         quant_h(7)
         group(5, HALF, "v")
+        store(5, HALF)
 
+        quarter = HALF // 2
         for i in (6, 7):
             for k in range(4):
-                group(i, HALF // 2 * k, "v" if k % 2 else "s", HALF // 2)
+                group(i, quarter * k, "sv"[k % 2], quarter)
+                if i == 7 and k > 1:
+                    store(i, quarter * k, quarter)
+                elif k % 2:
+                    store(i, quarter * (k - 1))

@@ -371,7 +371,7 @@ def tile_svftrandompatternsingularcoupling_d1p_kernel(
             quant_n(k)
         for i in range(4):
             close(i, 0, "s")
-            if i > 0:
+            if i > 1:
                 store(i, 0)
         for i in (6, 7):
             for g in (0, 1):
@@ -393,7 +393,10 @@ def tile_svftrandompatternsingularcoupling_d1p_kernel(
         quant_x(7)
         for i in range(1, 5):
             group(i, HALF, "s")
-            store(i, HALF)
+            if i == 1:
+                store(i, 0, N)
+            else:
+                store(i, HALF)
             if i > 2:
                 quant_h(i + 2)
             if i > 1:
@@ -409,7 +412,7 @@ def tile_svftrandompatternsingularcoupling_d1p_kernel(
         for i in (6, 7):
             for k in range(4):
                 group(i, quarter * k, "sv"[k % 2], quarter)
-                if i == 7 and k > 1:
+                if i == 7:
                     store(i, quarter * k, quarter)
                 elif k % 2:
                     store(i, quarter * (k - 1))

@@ -290,7 +290,8 @@ def tile_svftrandompatternsingularcoupling_d1p_kernel(
         nc.sync.dma_start(out=uw[0][:].bitcast(I32), in_=u_src[:, 0, :])
         load_scales(us, U_ROWS, u_scales)
         nc.sync.dma_start(out=uw[1][:].bitcast(I32), in_=u_src[:, 1, :])
-        nc.sync.dma_start(out=pat[:], in_=p_rows)
+        for h in (0, 1):
+            nc.sync.dma_start(out=pat[:, span(2 * R * h, 2 * R)], in_=p_rows[:, span(2 * R * h, 2 * R)])
         load_x(4, 1)
         for h in (0, 1):
             nc.sync.dma_start(out=mt[h][:], in_=m_rows[:, h, :])
@@ -371,7 +372,7 @@ def tile_svftrandompatternsingularcoupling_d1p_kernel(
             quant_n(k)
         for i in range(4):
             close(i, 0, "s")
-            if i > 1:
+            if i > 2:
                 store(i, 0)
         for i in (6, 7):
             for g in (0, 1):
@@ -393,7 +394,7 @@ def tile_svftrandompatternsingularcoupling_d1p_kernel(
         quant_x(7)
         for i in range(1, 5):
             group(i, HALF, "s")
-            if i == 1:
+            if i < 3:
                 store(i, 0, N)
             else:
                 store(i, HALF)

from contextlib import ExitStack

import concourse.mybir as mybir
from concourse.masks import make_identity

T, D, R, N = 1024, 1024, 512, 1024
FLOPS = 2 * (R * R * N + T * D * R + T * R * N + T * D * N)

P = 128
TILES = T // P
BANKS = 8
HALF = 512
KEEP_BELOW = 0.25
U_ROWS, V_ROWS, W_ROWS, N_ROWS = 4, 8, 12, 4

F32 = mybir.dt.float32
BF16 = mybir.dt.bfloat16
I32 = mybir.dt.int32
U32 = mybir.dt.uint32
U8 = mybir.dt.uint8
FP8 = mybir.dt.float8_e4m3fn
X4 = mybir.dt.float8_e4m3fn_x4
ALU = mybir.AluOpType
ACT = mybir.ActivationFunctionType


def tile_svftrandompatternsingularcoupling_d1p_kernel(
    tc, x_bytes, x_scale, w0_words, w0_scales, u_words, u_scales, m, pattern, vt_words, vt_scales, out
):
    nc = tc.nc
    with ExitStack() as ctx:
        keep = ctx.enter_context(tc.tile_pool(name="keep", bufs=1))
        psum = ctx.enter_context(tc.psum_pool(name="psum", bufs=1))

        def tile(name, shape, dtype):
            return keep.tile([P] + shape, dtype, align_bytes=256, name=name)

        xb = tile("xb", [TILES, D], U8)
        xs = tile("xs", [TILES * 8], F32)
        pat = tile("pat", [4 * R], BF16)
        mt = [tile("mt%d" % h, [2 * R], BF16) for h in (0, 1)]
        msk = [tile("msk%d" % h, [2 * R], BF16) for h in (0, 1)]
        uw = [tile("uw%d" % g, [R], U32) for g in (0, 1)]
        up = [tile("up%d" % g, [R], U32) for g in (0, 1)]
        us = tile("us", [2, R], U8)
        usp = tile("usp", [2, R], U8)
        vw = tile("vw", [N], U32)
        vs = tile("vs", [1, N], U8)
        ww = [tile("ww%d" % h, [2, HALF], U32) for h in (0, 1)]
        ws = [tile("ws%d" % h, [2, HALF], U8) for h in (0, 1)]
        ident = tile("ident", [P], F32)
        pident = tile("pident", [P], F32)
        msb = tile("msb", [4 * R], BF16)
        msq = tile("msq", [R], U32)
        mss = tile("mss", [R], U8)
        nb = [tile("nb%d" % c, [4 * P], BF16) for c in range(N // P)]
        nq = tile("nq", [N], U32)
        nsc = tile("nsc", [N], U8)
        xw = [[tile("xw%d%d" % (i, g), [HALF], BF16) for g in (0, 1)] for i in range(TILES)]
        xg = [tile("xg%d" % i, [D], BF16) for i in range(TILES)]
        xq = [tile("xq%d" % i, [2 * P], U32) for i in range(TILES)]
        xsc = [tile("xsc%d" % i, [2 * P], U8) for i in range(TILES)]
        hb = [tile("hb%d" % i, [4 * P], BF16) for i in range(TILES)]
        hq = [tile("hq%d" % i, [P], U32) for i in range(TILES)]
        hs = [tile("hs%d" % i, [P], U8) for i in range(TILES)]
        osb = [tile("osb%d" % i, [N], F32) for i in range(TILES)]

        ctx.enter_context(tc.manual_schedule())

        x_rows = x_bytes.rearrange("(p i) k -> p i k", i=TILES)
        m_rows = m.rearrange("(p h a) k -> p h (a k)", h=2, a=2)
        p_rows = pattern.rearrange("(p a) k -> p (a k)", a=4)
        out_rows = out.rearrange("(p i) n -> p i n", i=TILES)
        u_src = u_words.rearrange("g p n t -> p g (n t)").bitcast(I32)
        w_src = w0_words.rearrange("g p n t -> p g (n t)").bitcast(I32)
        v_src = vt_words[0].rearrange("p n t -> p (n t)").bitcast(I32)

        def span(start, width):
            return slice(start, start + width)


        def load_x(i, count):
            nc.sync.dma_start(out=xb[:, i : i + count, :], in_=x_rows[:, i : i + count, :])

        def load_scales(plane, first, scales):
            rows = scales.rearrange("g (q r) n -> r q g n", r=4)
            for r in range(4):
                nc.sync.dma_start(out=plane[first + r : P : 32, :, :].bitcast(I32), in_=rows[r].bitcast(I32))

        def load_w(h, parts):
            cols = span(HALF * h, HALF)
            load_scales(ws[h], W_ROWS, w0_scales[:, :, cols])
            for gs in parts:
                nc.sync.dma_start(out=ww[h][:, gs, :].bitcast(I32), in_=w_src[:, gs, cols])

        def load_v(h):
            cols = span(HALF * h, HALF)
            nc.sync.dma_start(out=vw[:, cols].bitcast(I32), in_=v_src[:, cols])


        live = {}
        idle = list(range(BANKS))

        def take(key):
            b = idle.pop(0)
            live[key] = (b, psum.tile([P, HALF], F32, tag="bank%d" % b, name="bank"))
            return live[key][1]

        def bank(key):
            return live[key][1] if key in live else take(key)

        def empty(key, eng, dst, view, last=True):
            b, acc = live[key]
            if eng == "v":
                nc.vector.tensor_copy(out=dst, in_=view(acc))
            else:
                nc.scalar.copy(out=dst, in_=view(acc))
            if last:
                idle.append(b)

        def warm(src, reps):
            acc = take("warm")
            cols = src.shape[1]
            rhs = src.unsqueeze(1).to_broadcast([P, reps, cols])
            dst = acc[:, 0 : reps * cols].rearrange("p (a c) -> p a c", a=reps)
            nc.tensor.matmul(dst, lhsT=src[:, 0:P], rhs=rhs, start=True, stop=True)
            idle.append(live["warm"][0])

        def mx(acc, lhs, rhs, start, stop):
            nc.tensor.matmul_mx(
                out=acc,
                lhsT=lhs[0].bitcast(X4),
                lhsT_scale=lhs[1],
                rhs=rhs[0].bitcast(X4),
                rhs_scale=rhs[1],
                start=start,
                stop=stop,
            )


        widened_by = {}

        def widen(i, g, eng):
            widened_by[i, g] = eng
            pairs = xw[i][g][:].rearrange("p (u c e) -> p c u e", u=2, e=2)
            for b in range(4):
                j = 4 * g + b
                src = xb[:, i, span(P * j, P)].bitcast(FP8)
                sc = xs[:, span(8 * i + j, 1)]
                if eng == "v":
                    nc.vector.tensor_scalar(
                        out=pairs[:, span(32 * b, 32), :, :],
                        in0=src.rearrange("p (c u e) -> p c u e", u=2, e=2),
                        scalar1=sc,
                        scalar2=None,
                        op0=ALU.mult,
                    )
                else:
                    nc.scalar.activation(out=xw[i][g][:, span(P * b, P)], in_=src, func=ACT.Copy, scale=sc)

        def x_bank(i, g):
            return ("tr", i, g if i == 0 else 0)

        def turn_x(i, halves=(0, 1)):
            for g in halves:
                tr = bank(x_bank(i, g))
                words = xw[i][g][:].bitcast(F32)
                for u in (0, 1):
                    src = words[:, span(P * u, P)] if widened_by[i, g] == "v" else words[:, u : 2 * P : 2]
                    nc.tensor.transpose(tr[:, span(P * (2 * g + u), P)], src, ident[:])

        def copy_x(i, eng, g0=0, g1=2):
            dst = xg[i][:].bitcast(F32).rearrange("p (g c u) -> p g c u", g=2, u=2)[:, g0:g1]
            view = lambda acc: acc[:].rearrange("p (g u c) -> p g c u", g=2, u=2)[:, g0:g1]
            empty(x_bank(i, g0), eng, dst, view, g1 == 2 or i == 0)

        def quant_x(i, g0=0, g1=2):
            words = slice(P * g0, P * g1)
            src = xg[i][:, HALF * g0 : HALF * g1]
            nc.vector.quantize_mx(out=xq[i][:, words].bitcast(X4), scales=xsc[i][:, words], in_=src)

        def x_operand(i, g):
            return xq[i][:, span(P * g, P)], xsc[i][:, span(P * g, P)]


        def permute_u(g):
            nc.vector.tensor_copy(
                out=up[g][:].bitcast(I32).rearrange("p (t q j) -> p t q j", t=4, q=16),
                in_=uw[g][:].bitcast(I32).rearrange("p (q t j) -> p t q j", q=16, t=4),
            )

        def permute_u_scales():
            nc.vector.tensor_copy(
                out=usp[:].bitcast(I32).rearrange("p g (t q j) -> p g t q j", t=4, q=16),
                in_=us[:].bitcast(I32).rearrange("p g (q t j) -> p g t q j", q=16, t=4),
            )


        def by_word(t):
            return t.rearrange("p (c u e) -> p u c e", u=2, e=2)

        def mask_test(h):
            dst = msk[h][:].rearrange("p (u c e) -> p u c e", u=2, e=2)
            src = by_word(pat[:, span(2 * R * h, 2 * R)])
            nc.vector.tensor_scalar(out=dst, in0=src, scalar1=KEEP_BELOW, scalar2=None, op0=ALU.is_lt)

        def mask_apply(h, u0=0, u1=2):
            dst = msk[h][:].rearrange("p (u c e) -> p u c e", u=2, e=2)[:, u0:u1]
            nc.vector.tensor_tensor(out=dst, in0=dst, in1=by_word(mt[h][:])[:, u0:u1], op=ALU.mult)

        def turn_m(h):
            tr = take(("trm", h))
            words = msk[h][:].bitcast(F32)
            for s in range(4):
                nc.tensor.transpose(tr[:, span(P * s, P)], words[:, span(P * s, P)], pident[:])

        def copy_m(h, eng, parts):
            dst = msb[:].bitcast(F32).rearrange("p (c a u) -> p c a u", a=4, u=2)
            for part in range(parts):
                cols = span(P // parts * part, P // parts)
                view = lambda acc: acc[:].rearrange("p (u a c) -> p c a u", a=2, u=2)[:, cols]
                empty(("trm", h), eng, dst[:, cols, span(2 * h, 2), :], view, part == parts - 1)

        def quant_m(t):
            cols = span(P * t, P)
            nc.vector.quantize_mx(out=msq[:, cols].bitcast(X4), scales=mss[:, cols], in_=msb[:, span(R * t, R)])


        def interleave(key, eng, dst):
            view = lambda acc: acc[:].rearrange("p (t n) -> p n t", t=4)
            empty(key, eng, dst[:].rearrange("p (n t) -> p n t", t=4), view)

        def mm_n(blocks):
            for t in range(4):
                rows = span(P * t, P)
                for c in blocks:
                    cols = span(P * c, P)
                    rhs = (vw[:, cols], vs[V_ROWS:P, 0, cols])
                    mx(bank(("n", c))[:, rows], (msq[:, rows], mss[:, rows]), rhs, True, True)

        def quant_n(c):
            cols = span(P * c, P)
            nc.vector.quantize_mx(out=nq[:, cols].bitcast(X4), scales=nsc[N_ROWS:P, cols], in_=nb[c][:])

        def mm_h(i):
            acc = take(("h", i))
            for g in (0, 1):
                for t in range(4):
                    rows = span(P * t, P)
                    lhs = (up[g][:, rows], usp[U_ROWS:P, g, rows])
                    mx(acc[:, rows], lhs, x_operand(i, g), (g, t) == (0, 0), (g, t) == (1, 3))

        def quant_h(i):
            nc.vector.quantize_mx(out=hq[i][:].bitcast(X4), scales=hs[i][:], in_=hb[i][:])


        def mm_b(i, c0, width=HALF, halves=(0, 1)):
            h, cols = c0 // HALF, span(c0 % HALF, width)
            for g in halves:
                rhs = (ww[h][:, g, cols], ws[h][W_ROWS:P, g, cols])
                mx(bank(("o", i, c0))[:, 0:width], x_operand(i, g), rhs, g == 0, False)

        def close(i, c0, eng, width=HALF):
            cols = span(c0, width)
            mx(bank(("o", i, c0))[:, 0:width], (hq[i][:], hs[i][:]), (nq[:, cols], nsc[N_ROWS:P, cols]), False, True)
            empty(("o", i, c0), eng, osb[i][:, cols], lambda acc: acc[:, 0:width])

        def group(i, c0, eng, width=HALF):
            mm_b(i, c0, width)
            close(i, c0, eng, width)

        def store(i, c0, width=HALF):
            cols = span(c0, width)
            nc.sync.dma_start(out=out_rows[:, i, cols], in_=osb[i][:, cols])


        for plane in (us, vs, ws[0], ws[1]):
            nc.vector.memset(plane[:].bitcast(I32), 0)
        warm(vs[:, 0, :].bitcast(F32), 2)
        make_identity(nc, ident[:])
        nc.scalar.copy(
            out=pident[:].rearrange("p (t q b) -> p t q b", t=4, q=16),
            in_=ident[:].rearrange("p (q t b) -> p t q b", q=16, t=4),
        )

        nc.sync.dma_start(out=xs[:], in_=x_scale.rearrange("(p i) j -> p (i j)", i=TILES))
        load_x(0, 1)
        load_x(1, 1)
        load_x(2, 2)
        nc.sync.dma_start(out=uw[0][:].bitcast(I32), in_=u_src[:, 0, :])
        load_scales(us, U_ROWS, u_scales)
        nc.sync.dma_start(out=uw[1][:].bitcast(I32), in_=u_src[:, 1, :])
        for h in (0, 1):
            nc.sync.dma_start(out=pat[:, span(2 * R * h, 2 * R)], in_=p_rows[:, span(2 * R * h, 2 * R)])
        load_x(4, 1)
        for h in (0, 1):
            nc.sync.dma_start(out=mt[h][:], in_=m_rows[:, h, :])
        load_w(0, (slice(0, 1), slice(1, 2)))
        load_v(0)
        load_scales(vs, V_ROWS, vt_scales)
        load_v(1)
        load_x(5, 3)
        load_w(1, (slice(0, 2),))

        for i in range(4):
            widen(i, 0, "v")
            widen(i, 1, "s" if i in (1, 2) else "v")
        for i in range(4):
            turn_x(i, (0,))
            if i == 0:
                warm(ident[:].bitcast(BF16), 2)
            turn_x(i, (1,))
            if i > 0:
                warm(ident[:].bitcast(BF16), 2 - i // 2)
            for g in (0, 1):
                copy_x(i, "s", g, g + 1)
        permute_u(0)
        permute_u_scales()
        quant_x(0, 0, 1)
        permute_u(1)
        quant_x(0, 1, 2)
        for g in (0, 1):
            quant_x(1, g, g + 1)
        widen(4, 0, "s")
        for i in (2, 3):
            quant_x(i, 0, 1)
            mask_test(i - 2)
            quant_x(i, 1, 2)
        for i in range(4):
            mm_h(i)
            interleave(("h", i), "s", hb[i])

        turn_x(4, (0,))
        mask_apply(0)
        turn_m(0)
        for u in (0, 1):
            mask_apply(1, u, u + 1)
        turn_m(1)
        widen(4, 1, "v")
        turn_x(4, (1,))
        quant_h(0)
        copy_m(0, "v", 2)
        copy_m(1, "s", 4)
        copy_x(4, "s")
        for g in (0, 1):
            for i in range(3 - g):
                mm_b(i, 0, halves=(g,))
        quant_h(1)
        for t in range(4):
            quant_m(t)
        for g in (0, 1):
            quant_x(4, g, g + 1)
        quant_h(2)
        quant_h(3)

        mm_n((0, 1))
        for c in range(N // P):
            if c > 1:
                mm_n((c,))
            interleave(("n", c), "v" if c in (1, 3, 5) else "s", nb[c])
            if c == 3:
                mm_h(4)
                mm_b(2, 0, halves=(1,))
                interleave(("h", 4), "s", hb[4])
                for k in range(4):
                    quant_n(k)
                widen(5, 0, "v")
        mm_b(3, 0)
        quant_h(4)
        widen(5, 1, "v")
        for k in range(4, 8):
            quant_n(k)
        for i in range(4):
            close(i, 0, "s")
            if i > 2:
                store(i, 0)
        for i in (6, 7):
            for g in (0, 1):
                widen(i, g, "v")
        group(4, 0, "s")
        store(4, 0)
        group(0, HALF, "s")
        store(0, 0, N)

        for i in (5, 6, 7):
            turn_x(i)
        for g in (0, 1):
            copy_x(5, "v", g, g + 1)
        copy_x(6, "s")
        for g in (0, 1):
            quant_x(5, g, g + 1)
        copy_x(7, "v")
        quant_x(6)
        quant_x(7)
        for i in range(1, 5):
            group(i, HALF, "s")
            if i < 3:
                store(i, 0, N)
            else:
                store(i, HALF)
            if i > 2:
                quant_h(i + 2)
            if i > 1:
                mm_h(i + 3)
                interleave(("h", i + 3), "v", hb[i + 3])
        group(5, 0, "s")
        store(5, 0)
        quant_h(7)
        group(5, HALF, "v")
        store(5, HALF)

        quarter = HALF // 2
        for i in (6, 7):
            for k in range(4):
                group(i, quarter * k, "sv"[k % 2], quarter)
                if i == 7:
                    store(i, quarter * k, quarter)
                elif k % 2:
                    store(i, quarter * (k - 1))
